import numpy as np
import ml_dtypes


def mxq(x, axis, fmt="e4m3"):
    dtype, down = {"e4m3": (ml_dtypes.float8_e4m3fn, 7), "e5m2": (ml_dtypes.float8_e5m2, 14)}[fmt]
    v = np.moveaxis(np.asarray(x, np.float32).astype(ml_dtypes.bfloat16).astype(np.float64), axis, -1)
    blocks = v.reshape(v.shape[:-1] + (-1, 32))
    amax = np.abs(blocks).max(-1, keepdims=True)
    byte = np.maximum(np.where(amax > 0, np.frexp(amax)[1] - 1 + 127, 0) - down, 1)
    scale = np.exp2(byte - 127.0)
    codes = (blocks / scale).astype(np.float32).astype(dtype).astype(np.float64)
    return np.moveaxis((codes * scale).reshape(v.shape), -1, axis)


WIDE = False


def mx_kscale(k):
    if not WIDE:
        return np.ones(k)
    levels = np.array([18, -18])
    if k % 512:
        return np.exp2(np.random.permutation(np.resize(levels, k // 32))).repeat(32)
    a = np.empty((k // 512, 16))
    for p in range(k // 512):
        a[p, :8] = np.random.permutation(np.resize(levels, 8))
        for g in range(8):
            far = levels[np.abs(levels - a[p, g]) >= 10]
            a[p, g + 8] = far[np.random.randint(len(far))]
    return np.exp2(a.ravel()).repeat(32)


def f64(x):
    return np.asarray(x).astype(np.float64)


def striped(idx):
    return np.tile(np.asarray(idx).reshape(-1, 16).T, (8, 1)).astype(np.uint16)


def unstriped(offs):
    return offs[:16].T.reshape(-1).astype(np.int64)


E2M1 = np.array([0.0, 0.5, 1.0, 1.5, 2.0, 3.0, 4.0, 6.0, -0.0, -0.5, -1.0, -1.5, -2.0, -3.0, -4.0, -6.0])


def pack_weight(w, fmt):
    k, n = w.shape
    w = f64(np.asarray(w, np.float32).astype(ml_dtypes.bfloat16)).reshape(k // 32, 32, n)
    amax = np.abs(w).max(1)
    if fmt == "e4m3":
        byte = np.frexp(amax)[1] - 1 + 127 - 7
    else:
        mant, ex = np.frexp(amax / 6.0)
        byte = np.where(mant > 0.5, ex, ex - 1) + 127
    byte = np.clip(np.where(amax > 0, byte, 1), 1, 254)
    scaled = (w * np.exp2(127.0 - byte)[:, None, :]).reshape(k, n).astype(np.float32)
    by_word = np.ascontiguousarray(scaled.reshape(k // 512, 128, 4, n).transpose(0, 1, 3, 2))
    if fmt == "e4m3":
        words = by_word.astype(ml_dtypes.float8_e4m3fn).view(np.uint8)
    else:
        c = by_word.astype(ml_dtypes.float4_e2m1fn).view(np.uint8) & 0xF
        words = (c[..., 0::2] | (c[..., 1::2] << 4)).reshape(k // 512, 128, 2 * n)
    return np.ascontiguousarray(words), np.ascontiguousarray(byte.astype(np.uint8).reshape(k // 512, 16, n))


def unpack_weight(words, scales, fmt):
    g, _, n = scales.shape
    words = np.ascontiguousarray(words).reshape(g, 128, n, -1)
    if fmt == "e4m3":
        vals = words.view(ml_dtypes.float8_e4m3fn).astype(np.float64)
    else:
        nib = np.empty((g, 128, n, 4), np.uint8)
        nib[..., 0::2] = words & 0xF
        nib[..., 1::2] = words >> 4
        vals = E2M1[nib]
    vals = vals * np.repeat(np.exp2(scales.astype(np.float64) - 127.0), 8, axis=1)[..., None]
    return vals.transpose(0, 1, 3, 2).reshape(g * 512, n)


B, N, T, D, R = 1, 512, 2048, 1024, 512


def setup_inputs():
    n = np.random.standard_normal
    idx = np.random.permutation(T)[:B * N]
    s = mx_kscale(D)[:, None]
    z = mx_kscale(R)[:, None]
    x = n((B, D, R))
    wp = pack_weight(n((D, T)) * (1.00 / np.sqrt(D)) / s, "e2m1")
    return {
        "xT": (x * s).astype(np.float32),
        "w_words": np.ascontiguousarray(wp[0].reshape(1, 2, 128, T, 2).transpose(0, 2, 3, 1, 4)).reshape(1, 128, T, 4),
        "w_scales": wp[1],
        "y": n((B, R, N)).astype(np.float32),
        "wt": (np.random.uniform(0.5, 1.5, (B, R, 1)) * 1.0 / np.sqrt(R) * z).astype(np.float32),
        "xm": (x.transpose(0, 2, 1) / z).astype(np.float32),
        "offs": striped(idx),
    }


def reference(xT, w_words, w_scales, y, wt, xm, offs):
    idx = unstriped(offs)
    w = unpack_weight(w_words.reshape(1, 128, T, 2, 2).transpose(0, 3, 1, 2, 4).reshape(2, 128, 2 * T), w_scales, "e2m1")
    pick = lambda x: x[:, idx].reshape(x.shape[0], B, N).transpose(1, 0, 2)
    a = mxq(f64(xT), 1, "e4m3").transpose(0, 2, 1) @ pick(w)
    g = f64(wt) * np.minimum(np.maximum(a - f64(y), -1.0), 1.0)
    dw = mxq(f64(xm), 1, "e4m3").transpose(0, 2, 1) @ mxq(g, 1, "e5m2")
    gw = np.zeros((D, T))
    gw[:, idx] = dw.transpose(1, 0, 2).reshape(D, B * N)
    return gw

@@ -1,0 +1,169 @@
+from contextlib import ExitStack
+
+import concourse.mybir as mybir
+
+N, T, D, R = 512, 2048, 1024, 512
+FLOPS = 2 * 2 * D * R * N
+
+F32 = mybir.dt.float32
+BF16 = mybir.dt.bfloat16
+I32 = mybir.dt.int32
+U32 = mybir.dt.uint32
+U16 = mybir.dt.uint16
+U8 = mybir.dt.uint8
+E4M3 = mybir.dt.float8_e4m3fn_x4
+E5M2 = mybir.dt.float8_e5m2_x4
+E2M1 = mybir.dt.float4_e2m1fn_x4
+ALU = mybir.AluOpType
+ACT = mybir.ActivationFunctionType
+
+P = 128
+PACK = 4
+PASSES = D // (P * PACK)
+XM_CHUNK = 256
+WINDOWS = 3
+
+
+def tile_attend_ghub_w_kernel(tc, xT, w_words, w_scales, y, wt, xm, offs, out):
+    nc = tc.nc
+    with ExitStack() as ctx:
+        held = ctx.enter_context(tc.tile_pool(name="held", bufs=1))
+        ring = ctx.enter_context(tc.tile_pool(name="ring", bufs=3))
+        psum = ctx.enter_context(tc.psum_pool(name="psum", bufs=1))
+        psum_ring = ctx.enter_context(tc.psum_pool(name="psum_ring", bufs=4))
+
+        offsets = held.tile([P, N // 16], U16, name="offsets")
+        nc.sync.dma_start(offsets[:], offs)
+
+        table_scales = held.tile([P, PASSES, T // 4], I32, name="table_scales", align_bytes=64)
+        nc.vector.memset(table_scales[:], 0)
+
+        table_words = held.tile([P, T], I32, name="table_words", align_bytes=64)
+        nc.sync.dma_start(table_words[:], w_words[0].rearrange("p t b -> p (t b)").bitcast(I32))
+        scale_rows = w_scales.bitcast(I32).rearrange("o f t -> f o t")
+        for b in range(4):
+            nc.sync.dma_start(table_scales[b:P:32, :, :], scale_rows[b:16:4, :, :])
+        w_row = held.tile([P, PACK], F32, name="w_row")
+        nc.sync.dma_start(w_row[:], wt[0].rearrange("(p t) o -> p (t o)", t=PACK))
+
+        x_raw = []
+        for g in range(PASSES):
+            raw = held.tile([P, PACK, R], F32, name="x_raw%d" % g)
+            nc.sync.dma_start(raw[:], xT[0, g * 512:(g + 1) * 512, :].rearrange("(p j) r -> p j r", j=PACK))
+            x_raw.append(raw)
+        y_rows = y[0].rearrange("(p t) i -> p t i", t=PACK)
+        y_raw = []
+        for u in range(2):
+            raw = held.tile([P, 2, N], F32, name="y_raw%d" % u)
+            nc.sync.dma_start(raw[:], y_rows[:, 2 * u:2 * u + 2, :])
+            y_raw.append(raw)
+        xm_rows = xm[0].rearrange("(p t) d -> p t d", t=PACK)
+        xm_raw = []
+        for c in range(D // XM_CHUNK):
+            raw = held.tile([P, PACK, XM_CHUNK], F32, name="xm_raw%d" % c)
+            nc.sync.dma_start(raw[:], xm_rows[:, :, c * XM_CHUNK:(c + 1) * XM_CHUNK])
+            xm_raw.append(raw)
+
+        windows = []
+        for k in range(WINDOWS):
+            window = held.tile([P, T], F32, name="window%d" % k)
+            nc.vector.memset(window[:], 0.0)
+            windows.append(window)
+
+        w_hi = held.tile([P, PACK], F32, name="w_hi")
+        w_lo = held.tile([P, PACK], F32, name="w_lo")
+        nc.scalar.activation(w_hi[:], w_row[:], ACT.Abs)
+        nc.scalar.activation(w_lo[:], w_hi[:], ACT.Copy, scale=-1.0)
+
+        item_scales = []
+        for g in range(PASSES):
+            plane = held.tile([P, N], U8, name="item_scales%d" % g, align_bytes=64)
+            nc.vector.tensor_copy(plane[:], table_scales[:, g, :].bitcast(U8).indirect(offsets[:]))
+            item_scales.append(plane)
+        item_pairs = held.tile([P, N], U32, name="item_pairs", align_bytes=64)
+        nc.vector.tensor_copy(item_pairs[:], table_words[:].bitcast(U32).indirect(offsets[:]))
+        item_words = held.tile([P, PASSES, N], U16, name="item_words", align_bytes=64)
+        nc.vector.tensor_copy(item_words[:], item_pairs[:].bitcast(U16).rearrange("p (n o) -> p o n", o=PASSES))
+
+        scores = [psum.tile([P, N], F32, name="scores%d" % t) for t in range(PACK)]
+
+        def interleave_x(g, u, on_vector):
+            grouped = held.tile([P, 2, P, PACK], BF16, name="x_grouped%d_%d" % (g, u), align_bytes=64)
+            src = x_raw[g][:].rearrange("p j (m t) -> p m t j", t=PACK)[:, :, 2 * u:2 * u + 2, :]
+            dst = grouped[:].rearrange("p t m j -> p m t j")
+            if on_vector:
+                nc.vector.tensor_copy(dst, src)
+            else:
+                nc.scalar.copy(dst, src)
+            return grouped
+
+        def first_product(g, u, grouped):
+            codes = held.tile([P, 2 * P], U32, name="x_codes%d_%d" % (g, u), align_bytes=64)
+            scales = held.tile([P, 2 * P], U8, name="x_scales%d_%d" % (g, u), align_bytes=64)
+            nc.vector.quantize_mx(codes[:].bitcast(E4M3), scales[:], grouped[:].rearrange("p t m j -> p (t m j)"))
+            for v in range(2):
+                cols = slice(v * P, (v + 1) * P)
+                nc.tensor.matmul_mx(
+                    scores[2 * u + v][:],
+                    lhsT=codes[:, cols].bitcast(E4M3), lhsT_scale=scales[:, cols],
+                    rhs=item_words[:, g, :].bitcast(E2M1), rhs_scale=item_scales[g][:],
+                    start=(g == 0), stop=(g == PASSES - 1),
+                )
+
+        a0 = interleave_x(0, 0, False)
+        a1 = interleave_x(0, 1, True)
+        first_product(0, 0, a0)
+        first_product(0, 1, a1)
+        b0 = interleave_x(1, 0, True)
+        b1 = interleave_x(1, 1, False)
+        first_product(1, 0, b0)
+        first_product(1, 1, b1)
+
+        yw = []
+        for t in range(PACK):
+            tile = held.tile([P, N], F32, name="yw%d" % t)
+            nc.scalar.activation(tile[:], y_raw[t // 2][:, t % 2, :], ACT.Copy, scale=w_row[:, t:t + 1])
+            yw.append(tile)
+
+        g_rows = held.tile([P, PACK, N], BF16, name="g_rows", align_bytes=64)
+        resid = [held.tile([P, N], F32, name="resid%d" % t) for t in range(PACK)]
+
+        def residual(t):
+            nc.vector.scalar_tensor_tensor(resid[t][:], scores[t][:], w_row[:, t:t + 1], yw[t][:], ALU.mult, ALU.subtract)
+
+        def clip(t):
+            nc.vector.tensor_scalar(g_rows[:, t, :], resid[t][:], w_lo[:, t:t + 1], w_hi[:, t:t + 1], ALU.max, ALU.min)
+
+        residual(0)
+        for t in range(1, PACK):
+            residual(t)
+            clip(t - 1)
+        clip(PACK - 1)
+
+        g_grouped = held.tile([P, N, PACK], BF16, name="g_grouped", align_bytes=64)
+        nc.vector.tensor_copy(g_grouped[:], g_rows[:].rearrange("p t i -> p i t"))
+        g_codes = held.tile([P, N], U32, name="g_codes", align_bytes=64)
+        g_scales = held.tile([P, N], U8, name="g_scales", align_bytes=64)
+        nc.vector.quantize_mx(g_codes[:].bitcast(E5M2), g_scales[:], g_grouped[:].rearrange("p i t -> p (i t)"))
+
+        for c in range(D // XM_CHUNK):
+            grouped = held.tile([P, XM_CHUNK, PACK], BF16, name="xm_grouped%d" % c, align_bytes=64)
+            nc.scalar.copy(grouped[:], xm_raw[c][:].rearrange("p t d -> p d t"))
+            codes = held.tile([P, XM_CHUNK], U32, name="xm_codes%d" % c, align_bytes=64)
+            scales = held.tile([P, XM_CHUNK], U8, name="xm_scales%d" % c, align_bytes=64)
+            nc.vector.quantize_mx(codes[:].bitcast(E4M3), scales[:], grouped[:].rearrange("p d t -> p (d t)"))
+            for v in range(XM_CHUNK // P):
+                k = c * (XM_CHUNK // P) + v
+                cols = slice(v * P, (v + 1) * P)
+                grad = psum_ring.tile([P, N], F32, name="grad")
+                nc.tensor.matmul_mx(
+                    grad[:],
+                    lhsT=codes[:, cols].bitcast(E4M3), lhsT_scale=scales[:, cols],
+                    rhs=g_codes[:].bitcast(E5M2), rhs_scale=g_scales[:],
+                    start=True, stop=True,
+                )
+                dense = ring.tile([P, N], F32, name="dense")
+                nc.scalar.copy(dense[:], grad[:])
+                window = windows[k % WINDOWS]
+                nc.vector.tensor_copy(window[:].indirect(offsets[:]), dense[:])
+                nc.sync.dma_start(out[k * P:(k + 1) * P, :], window[:])

@@ -22,6 +22,7 @@ PACK = 4
 PASSES = D // (P * PACK)
 XM_CHUNK = 256
 WINDOWS = 3
+G_SPLIT = 352
 
 
 def tile_attend_ghub_w_kernel(tc, xT, w_words, w_scales, y, wt, xm, offs, out):
@@ -36,7 +37,7 @@ def tile_attend_ghub_w_kernel(tc, xT, w_words, w_scales, y, wt, xm, offs, out):
         nc.sync.dma_start(offsets[:], offs)
 
         table_scales = held.tile([P, PASSES, T // 4], I32, name="table_scales", align_bytes=64)
-        nc.vector.memset(table_scales[:], 0)
+        nc.gpsimd.memset(table_scales[:], 0)
 
         table_words = held.tile([P, T], I32, name="table_words", align_bytes=64)
         nc.sync.dma_start(table_words[:], w_words[0].rearrange("p t b -> p (t b)").bitcast(I32))
@@ -65,9 +66,9 @@ def tile_attend_ghub_w_kernel(tc, xT, w_words, w_scales, y, wt, xm, offs, out):
             xm_raw.append(raw)
 
         windows = []
-        for k in range(WINDOWS):
+        for k in range(WINDOWS - 1):
             window = held.tile([P, T], F32, name="window%d" % k)
-            nc.vector.memset(window[:], 0.0)
+            nc.gpsimd.memset(window[:], 0.0)
             windows.append(window)
 
         w_hi = held.tile([P, PACK], F32, name="w_hi")
@@ -75,13 +76,13 @@ def tile_attend_ghub_w_kernel(tc, xT, w_words, w_scales, y, wt, xm, offs, out):
         nc.scalar.activation(w_hi[:], w_row[:], ACT.Abs)
         nc.scalar.activation(w_lo[:], w_hi[:], ACT.Copy, scale=-1.0)
 
+        item_pairs = held.tile([P, N], U32, name="item_pairs", align_bytes=64)
+        nc.vector.tensor_copy(item_pairs[:], table_words[:].bitcast(U32).indirect(offsets[:]))
         item_scales = []
         for g in range(PASSES):
             plane = held.tile([P, N], U8, name="item_scales%d" % g, align_bytes=64)
             nc.vector.tensor_copy(plane[:], table_scales[:, g, :].bitcast(U8).indirect(offsets[:]))
             item_scales.append(plane)
-        item_pairs = held.tile([P, N], U32, name="item_pairs", align_bytes=64)
-        nc.vector.tensor_copy(item_pairs[:], table_words[:].bitcast(U32).indirect(offsets[:]))
         item_words = held.tile([P, PASSES, N], U16, name="item_words", align_bytes=64)
         nc.vector.tensor_copy(item_words[:], item_pairs[:].bitcast(U16).rearrange("p (n o) -> p o n", o=PASSES))
 
@@ -89,8 +90,8 @@ def tile_attend_ghub_w_kernel(tc, xT, w_words, w_scales, y, wt, xm, offs, out):
 
         def interleave_x(g, u, on_vector):
             grouped = held.tile([P, 2, P, PACK], BF16, name="x_grouped%d_%d" % (g, u), align_bytes=64)
-            src = x_raw[g][:].rearrange("p j (m t) -> p m t j", t=PACK)[:, :, 2 * u:2 * u + 2, :]
-            dst = grouped[:].rearrange("p t m j -> p m t j")
+            src = x_raw[g][:].rearrange("p j (m t) -> p m j t", t=PACK)[:, :, :, 2 * u:2 * u + 2]
+            dst = grouped[:].rearrange("p t m j -> p m j t")
             if on_vector:
                 nc.vector.tensor_copy(dst, src)
             else:
@@ -140,18 +141,33 @@ def tile_attend_ghub_w_kernel(tc, xT, w_words, w_scales, y, wt, xm, offs, out):
             clip(t - 1)
         clip(PACK - 1)
 
-        g_grouped = held.tile([P, N, PACK], BF16, name="g_grouped", align_bytes=64)
-        nc.vector.tensor_copy(g_grouped[:], g_rows[:].rearrange("p t i -> p i t"))
-        g_codes = held.tile([P, N], U32, name="g_codes", align_bytes=64)
-        g_scales = held.tile([P, N], U8, name="g_scales", align_bytes=64)
-        nc.vector.quantize_mx(g_codes[:].bitcast(E5M2), g_scales[:], g_grouped[:].rearrange("p i t -> p (i t)"))
-
-        for c in range(D // XM_CHUNK):
+        def interleave_xm(c):
             grouped = held.tile([P, XM_CHUNK, PACK], BF16, name="xm_grouped%d" % c, align_bytes=64)
-            nc.scalar.copy(grouped[:], xm_raw[c][:].rearrange("p t d -> p d t"))
+            nc.scalar.copy(grouped[:].rearrange("p (e i) t -> p e t i", i=4), xm_raw[c][:].rearrange("p t (e i) -> p e t i", i=4))
+            return grouped
+
+        def quantize_xm(c, grouped):
             codes = held.tile([P, XM_CHUNK], U32, name="xm_codes%d" % c, align_bytes=64)
             scales = held.tile([P, XM_CHUNK], U8, name="xm_scales%d" % c, align_bytes=64)
             nc.vector.quantize_mx(codes[:].bitcast(E4M3), scales[:], grouped[:].rearrange("p d t -> p (d t)"))
+            return codes, scales
+
+        first_xm = quantize_xm(0, interleave_xm(0))
+
+        g_grouped = held.tile([P, N, PACK], BF16, name="g_grouped", tag="late", align_bytes=64)
+        g_dst = g_grouped[:].rearrange("p (e i) t -> p e t i", i=4)
+        g_src = g_rows[:].rearrange("p t (e i) -> p e t i", i=4)
+        nc.vector.tensor_copy(g_dst[:, :G_SPLIT // 4], g_src[:, :G_SPLIT // 4])
+        nc.scalar.copy(g_dst[:, G_SPLIT // 4:], g_src[:, G_SPLIT // 4:])
+        g_codes = held.tile([P, N], U32, name="g_codes", align_bytes=64)
+        g_scales = held.tile([P, N], U8, name="g_scales", align_bytes=64)
+        nc.vector.quantize_mx(g_codes[:].bitcast(E5M2), g_scales[:], g_grouped[:].rearrange("p i t -> p (i t)"))
+        window = held.tile([P, T], F32, name="window_late", tag="late", align_bytes=64)
+        nc.vector.memset(window[:], 0.0)
+        windows.append(window)
+
+        for c in range(D // XM_CHUNK):
+            codes, scales = first_xm if c == 0 else quantize_xm(c, interleave_xm(c))
             for v in range(XM_CHUNK // P):
                 k = c * (XM_CHUNK // P) + v
                 cols = slice(v * P, (v + 1) * P)

@@ -22,7 +22,6 @@ PACK = 4
 PASSES = D // (P * PACK)
 XM_CHUNK = 256
 WINDOWS = 3
-G_SPLIT = 352
 
 
 def tile_attend_ghub_w_kernel(tc, xT, w_words, w_scales, y, wt, xm, offs, out):
@@ -36,16 +35,18 @@ def tile_attend_ghub_w_kernel(tc, xT, w_words, w_scales, y, wt, xm, offs, out):
         offsets = held.tile([P, N // 16], U16, name="offsets")
         nc.sync.dma_start(offsets[:], offs)
 
-        table_scales = held.tile([P, PASSES, T // 4], I32, name="table_scales", align_bytes=64)
-        nc.gpsimd.memset(table_scales[:], 0)
+        table_scales = held.tile([P, T // 4], I32, name="table_scales", align_bytes=64)
+        nc.vector.memset(table_scales[:], 0)
+        moved_scales = held.tile([P, N // 4], I32, name="moved_scales", align_bytes=64)
+        nc.vector.memset(moved_scales[:], 0)
 
-        table_words = held.tile([P, T], I32, name="table_words", align_bytes=64)
-        nc.sync.dma_start(table_words[:], w_words[0].rearrange("p t b -> p (t b)").bitcast(I32))
-        scale_rows = w_scales.bitcast(I32).rearrange("o f t -> f o t")
-        for b in range(4):
-            nc.sync.dma_start(table_scales[b:P:32, :, :], scale_rows[b:16:4, :, :])
         w_row = held.tile([P, PACK], F32, name="w_row")
         nc.sync.dma_start(w_row[:], wt[0].rearrange("(p t) o -> p (t o)", t=PACK))
+        scale_rows = w_scales.bitcast(I32).rearrange("o (q b) t -> b q o t", b=4)
+        for b in range(4):
+            nc.sync.dma_start(table_scales[b:P:16, :], scale_rows[b])
+        table_words = held.tile([P, T], I32, name="table_words", align_bytes=64)
+        nc.sync.dma_start(table_words[:], w_words[0].rearrange("p t b -> p (t b)").bitcast(I32))
 
         x_raw = []
         for g in range(PASSES):
@@ -66,9 +67,9 @@ def tile_attend_ghub_w_kernel(tc, xT, w_words, w_scales, y, wt, xm, offs, out):
             xm_raw.append(raw)
 
         windows = []
-        for k in range(WINDOWS - 1):
+        for k in range(WINDOWS):
             window = held.tile([P, T], F32, name="window%d" % k)
-            nc.gpsimd.memset(window[:], 0.0)
+            nc.vector.memset(window[:], 0.0)
             windows.append(window)
 
         w_hi = held.tile([P, PACK], F32, name="w_hi")
@@ -76,13 +77,12 @@ def tile_attend_ghub_w_kernel(tc, xT, w_words, w_scales, y, wt, xm, offs, out):
         nc.scalar.activation(w_hi[:], w_row[:], ACT.Abs)
         nc.scalar.activation(w_lo[:], w_hi[:], ACT.Copy, scale=-1.0)
 
+        both_scales = held.tile([P, N], U8, name="both_scales", align_bytes=64)
+        nc.vector.tensor_copy(both_scales[:], table_scales[:].bitcast(U8).indirect(offsets[:]))
+        nc.gpsimd.dma_start(moved_scales[0:P - 16, :], both_scales[16:P, :].bitcast(I32))
+        item_scales = [both_scales[:], moved_scales[:].bitcast(U8)]
         item_pairs = held.tile([P, N], U32, name="item_pairs", align_bytes=64)
         nc.vector.tensor_copy(item_pairs[:], table_words[:].bitcast(U32).indirect(offsets[:]))
-        item_scales = []
-        for g in range(PASSES):
-            plane = held.tile([P, N], U8, name="item_scales%d" % g, align_bytes=64)
-            nc.vector.tensor_copy(plane[:], table_scales[:, g, :].bitcast(U8).indirect(offsets[:]))
-            item_scales.append(plane)
         item_words = held.tile([P, PASSES, N], U16, name="item_words", align_bytes=64)
         nc.vector.tensor_copy(item_words[:], item_pairs[:].bitcast(U16).rearrange("p (n o) -> p o n", o=PASSES))
 
@@ -107,7 +107,7 @@ def tile_attend_ghub_w_kernel(tc, xT, w_words, w_scales, y, wt, xm, offs, out):
                 nc.tensor.matmul_mx(
                     scores[2 * u + v][:],
                     lhsT=codes[:, cols].bitcast(E4M3), lhsT_scale=scales[:, cols],
-                    rhs=item_words[:, g, :].bitcast(E2M1), rhs_scale=item_scales[g][:],
+                    rhs=item_words[:, g, :].bitcast(E2M1), rhs_scale=item_scales[g],
                     start=(g == 0), stop=(g == PASSES - 1),
                 )
 
@@ -127,7 +127,7 @@ def tile_attend_ghub_w_kernel(tc, xT, w_words, w_scales, y, wt, xm, offs, out):
             yw.append(tile)
 
         g_rows = held.tile([P, PACK, N], BF16, name="g_rows", align_bytes=64)
-        resid = [held.tile([P, N], F32, name="resid%d" % t) for t in range(PACK)]
+        resid = [held.tile([P, N], F32, name="resid%d" % t, tag="xm_codes" if t == PACK - 2 else "resid%d" % t, align_bytes=64) for t in range(PACK)]
 
         def residual(t):
             nc.vector.scalar_tensor_tensor(resid[t][:], scores[t][:], w_row[:, t:t + 1], yw[t][:], ALU.mult, ALU.subtract)
@@ -142,29 +142,25 @@ def tile_attend_ghub_w_kernel(tc, xT, w_words, w_scales, y, wt, xm, offs, out):
         clip(PACK - 1)
 
         def interleave_xm(c):
-            grouped = held.tile([P, XM_CHUNK, PACK], BF16, name="xm_grouped%d" % c, align_bytes=64)
+            grouped = held.tile([P, XM_CHUNK, PACK], BF16, name="xm_grouped", align_bytes=64)
             nc.scalar.copy(grouped[:].rearrange("p (e i) t -> p e t i", i=4), xm_raw[c][:].rearrange("p t (e i) -> p e t i", i=4))
             return grouped
 
         def quantize_xm(c, grouped):
-            codes = held.tile([P, XM_CHUNK], U32, name="xm_codes%d" % c, align_bytes=64)
-            scales = held.tile([P, XM_CHUNK], U8, name="xm_scales%d" % c, align_bytes=64)
+            codes = held.tile([P, XM_CHUNK], U32, name="xm_codes", tag="xm_codes", align_bytes=64)
+            scales = held.tile([P, XM_CHUNK], U8, name="xm_scales", align_bytes=64)
             nc.vector.quantize_mx(codes[:].bitcast(E4M3), scales[:], grouped[:].rearrange("p d t -> p (d t)"))
             return codes, scales
 
         first_xm = quantize_xm(0, interleave_xm(0))
 
-        g_grouped = held.tile([P, N, PACK], BF16, name="g_grouped", tag="late", align_bytes=64)
+        g_grouped = held.tile([P, N, PACK], BF16, name="g_grouped", align_bytes=64)
         g_dst = g_grouped[:].rearrange("p (e i) t -> p e t i", i=4)
         g_src = g_rows[:].rearrange("p t (e i) -> p e t i", i=4)
-        nc.vector.tensor_copy(g_dst[:, :G_SPLIT // 4], g_src[:, :G_SPLIT // 4])
-        nc.scalar.copy(g_dst[:, G_SPLIT // 4:], g_src[:, G_SPLIT // 4:])
+        nc.vector.tensor_copy(g_dst, g_src)
         g_codes = held.tile([P, N], U32, name="g_codes", align_bytes=64)
         g_scales = held.tile([P, N], U8, name="g_scales", align_bytes=64)
         nc.vector.quantize_mx(g_codes[:].bitcast(E5M2), g_scales[:], g_grouped[:].rearrange("p i t -> p (i t)"))
-        window = held.tile([P, T], F32, name="window_late", tag="late", align_bytes=64)
-        nc.vector.memset(window[:], 0.0)
-        windows.append(window)
 
         for c in range(D // XM_CHUNK):
             codes, scales = first_xm if c == 0 else quantize_xm(c, interleave_xm(c))

@@ -22,50 +22,42 @@ PACK = 4
 PASSES = D // (P * PACK)
 XM_CHUNK = 256
 WINDOWS = 3
+HALF = N // 2
 
 
 def tile_attend_ghub_w_kernel(tc, xT, w_words, w_scales, y, wt, xm, offs, out):
     nc = tc.nc
     with ExitStack() as ctx:
         held = ctx.enter_context(tc.tile_pool(name="held", bufs=1))
-        ring = ctx.enter_context(tc.tile_pool(name="ring", bufs=3))
+        ring = ctx.enter_context(tc.tile_pool(name="ring", bufs=4))
         psum = ctx.enter_context(tc.psum_pool(name="psum", bufs=1))
         psum_ring = ctx.enter_context(tc.psum_pool(name="psum_ring", bufs=4))
 
         offsets = held.tile([P, N // 16], U16, name="offsets")
         nc.sync.dma_start(offsets[:], offs)
 
-        table_scales = held.tile([P, T // 4], I32, name="table_scales", align_bytes=64)
+        table_words = held.tile([P, T], I32, name="table_words", align_bytes=64)
+        nc.sync.dma_start(table_words[:], w_words[0].rearrange("p t b -> p (t b)").bitcast(I32))
+        table_scales = held.tile([P, T // 4], I32, name="table_scales", tag="scales_then_y", align_bytes=64)
         nc.vector.memset(table_scales[:], 0)
-        moved_scales = held.tile([P, N // 4], I32, name="moved_scales", align_bytes=64)
-        nc.vector.memset(moved_scales[:], 0)
-
-        w_row = held.tile([P, PACK], F32, name="w_row")
-        nc.sync.dma_start(w_row[:], wt[0].rearrange("(p t) o -> p (t o)", t=PACK))
         scale_rows = w_scales.bitcast(I32).rearrange("o (q b) t -> b q o t", b=4)
         for b in range(4):
             nc.sync.dma_start(table_scales[b:P:16, :], scale_rows[b])
-        table_words = held.tile([P, T], I32, name="table_words", align_bytes=64)
-        nc.sync.dma_start(table_words[:], w_words[0].rearrange("p t b -> p (t b)").bitcast(I32))
+        w_row = held.tile([P, PACK], F32, name="w_row")
+        nc.sync.dma_start(w_row[:], wt[0].rearrange("(p t) o -> p (t o)", t=PACK))
 
         x_raw = []
         for g in range(PASSES):
-            raw = held.tile([P, PACK, R], F32, name="x_raw%d" % g)
+            raw = held.tile([P, PACK, R], F32, name="x_raw%d" % g, tag="x%d_then_xm" % g)
             nc.sync.dma_start(raw[:], xT[0, g * 512:(g + 1) * 512, :].rearrange("(p j) r -> p j r", j=PACK))
             x_raw.append(raw)
-        y_rows = y[0].rearrange("(p t) i -> p t i", t=PACK)
-        y_raw = []
-        for u in range(2):
-            raw = held.tile([P, 2, N], F32, name="y_raw%d" % u)
-            nc.sync.dma_start(raw[:], y_rows[:, 2 * u:2 * u + 2, :])
-            y_raw.append(raw)
-        xm_rows = xm[0].rearrange("(p t) d -> p t d", t=PACK)
-        xm_raw = []
-        for c in range(D // XM_CHUNK):
-            raw = held.tile([P, PACK, XM_CHUNK], F32, name="xm_raw%d" % c)
-            nc.sync.dma_start(raw[:], xm_rows[:, :, c * XM_CHUNK:(c + 1) * XM_CHUNK])
-            xm_raw.append(raw)
 
+        moved_scales = held.tile([P, N // 4], I32, name="moved_scales", align_bytes=64)
+        nc.vector.memset(moved_scales[:], 0)
+        g_codes = held.tile([P, N], I32, name="g_codes", align_bytes=64)
+        g_scales = held.tile([P, N // 4], I32, name="g_scales", align_bytes=64)
+        nc.vector.memset(g_codes[:, HALF:], 0)
+        nc.vector.memset(g_scales[:, HALF // 4:], 0)
         windows = []
         for k in range(WINDOWS):
             window = held.tile([P, T], F32, name="window%d" % k)
@@ -77,14 +69,21 @@ def tile_attend_ghub_w_kernel(tc, xT, w_words, w_scales, y, wt, xm, offs, out):
         nc.scalar.activation(w_hi[:], w_row[:], ACT.Abs)
         nc.scalar.activation(w_lo[:], w_hi[:], ACT.Copy, scale=-1.0)
 
+        item_pairs = held.tile([P, N], U32, name="item_pairs", tag="pairs_then_y", align_bytes=64)
+        nc.vector.tensor_copy(item_pairs[:], table_words[:].bitcast(U32).indirect(offsets[:]))
         both_scales = held.tile([P, N], U8, name="both_scales", align_bytes=64)
         nc.vector.tensor_copy(both_scales[:], table_scales[:].bitcast(U8).indirect(offsets[:]))
-        nc.gpsimd.dma_start(moved_scales[0:P - 16, :], both_scales[16:P, :].bitcast(I32))
+        nc.sync.dma_start(moved_scales[0:P - 16, :], both_scales[16:P, :].bitcast(I32))
         item_scales = [both_scales[:], moved_scales[:].bitcast(U8)]
-        item_pairs = held.tile([P, N], U32, name="item_pairs", align_bytes=64)
-        nc.vector.tensor_copy(item_pairs[:], table_words[:].bitcast(U32).indirect(offsets[:]))
         item_words = held.tile([P, PASSES, N], U16, name="item_words", align_bytes=64)
         nc.vector.tensor_copy(item_words[:], item_pairs[:].bitcast(U16).rearrange("p (n o) -> p o n", o=PASSES))
+
+        y_rows = y[0].rearrange("(p t) i -> p t i", t=PACK)
+        xm_rows = xm[0].rearrange("(p t) d -> p t d", t=PACK)
+        y_raw0 = held.tile([P, PACK, HALF], F32, name="y_raw0", tag="scales_then_y", align_bytes=64)
+        nc.sync.dma_start(y_raw0[:], y_rows[:, :, :HALF])
+        xm_raw0 = held.tile([P, PACK, XM_CHUNK], F32, name="xm_raw0", tag="pairs_then_y", align_bytes=64)
+        nc.sync.dma_start(xm_raw0[:], xm_rows[:, :, :XM_CHUNK])
 
         scores = [psum.tile([P, N], F32, name="scores%d" % t) for t in range(PACK)]
 
@@ -115,67 +114,113 @@ def tile_attend_ghub_w_kernel(tc, xT, w_words, w_scales, y, wt, xm, offs, out):
         a1 = interleave_x(0, 1, True)
         first_product(0, 0, a0)
         first_product(0, 1, a1)
+        rest_raw = held.tile([P, PACK, D], F32, name="rest_raw", tag="x0_then_xm")
+        nc.sync.dma_start(rest_raw[:, :, :HALF], y_rows[:, :, HALF:])
+        for c in range(1, D // XM_CHUNK):
+            chunk = slice(c * XM_CHUNK, (c + 1) * XM_CHUNK)
+            nc.sync.dma_start(rest_raw[:, :, chunk], xm_rows[:, :, chunk])
+        y_raw = [y_raw0[:], rest_raw[:, :, :HALF]]
+        xm_raw = [xm_raw0[:]] + [rest_raw[:, :, c * XM_CHUNK:(c + 1) * XM_CHUNK] for c in range(1, D // XM_CHUNK)]
         b0 = interleave_x(1, 0, True)
         b1 = interleave_x(1, 1, False)
         first_product(1, 0, b0)
         first_product(1, 1, b1)
 
-        yw = []
-        for t in range(PACK):
-            tile = held.tile([P, N], F32, name="yw%d" % t)
-            nc.scalar.activation(tile[:], y_raw[t // 2][:, t % 2, :], ACT.Copy, scale=w_row[:, t:t + 1])
-            yw.append(tile)
+        def weigh_targets(h):
+            yw = held.tile([P, PACK, HALF], F32, name="yw%d" % h)
+            for t in range(PACK):
+                nc.scalar.activation(yw[:, t, :], y_raw[h][:, t, :], ACT.Copy, scale=w_row[:, t:t + 1])
+            return yw
 
-        g_rows = held.tile([P, PACK, N], BF16, name="g_rows", align_bytes=64)
-        resid = [held.tile([P, N], F32, name="resid%d" % t, tag="xm_codes" if t == PACK - 2 else "resid%d" % t, align_bytes=64) for t in range(PACK)]
+        def residual(h, t, resid, yw):
+            nc.vector.scalar_tensor_tensor(
+                resid, scores[t][:, h * HALF:(h + 1) * HALF], w_row[:, t:t + 1], yw[:, t, :], ALU.mult, ALU.subtract
+            )
 
-        def residual(t):
-            nc.vector.scalar_tensor_tensor(resid[t][:], scores[t][:], w_row[:, t:t + 1], yw[t][:], ALU.mult, ALU.subtract)
+        def clip(t, g_rows, resid):
+            nc.vector.tensor_scalar(g_rows[:, t, :], resid, w_lo[:, t:t + 1], w_hi[:, t:t + 1], ALU.max, ALU.min)
 
-        def clip(t):
-            nc.vector.tensor_scalar(g_rows[:, t, :], resid[t][:], w_lo[:, t:t + 1], w_hi[:, t:t + 1], ALU.max, ALU.min)
-
-        residual(0)
-        for t in range(1, PACK):
-            residual(t)
-            clip(t - 1)
-        clip(PACK - 1)
+        def interleaved(grouped, rows):
+            return grouped[:].rearrange("p (e i) t -> p e t i", i=4), rows.rearrange("p t (e i) -> p e t i", i=4)
 
         def interleave_xm(c):
-            grouped = held.tile([P, XM_CHUNK, PACK], BF16, name="xm_grouped", align_bytes=64)
-            nc.scalar.copy(grouped[:].rearrange("p (e i) t -> p e t i", i=4), xm_raw[c][:].rearrange("p t (e i) -> p e t i", i=4))
+            grouped = held.tile([P, XM_CHUNK, PACK], BF16, name="xm_grouped%d" % c, tag="xm_grouped", align_bytes=64)
+            nc.scalar.copy(*interleaved(grouped, xm_raw[c]))
             return grouped
 
         def quantize_xm(c, grouped):
-            codes = held.tile([P, XM_CHUNK], U32, name="xm_codes", tag="xm_codes", align_bytes=64)
-            scales = held.tile([P, XM_CHUNK], U8, name="xm_scales", align_bytes=64)
+            codes = held.tile([P, XM_CHUNK], U32, name="xm_codes%d" % c, tag="xm_codes", align_bytes=64)
+            scales = held.tile([P, XM_CHUNK], U8, name="xm_scales%d" % c, tag="xm_scales", align_bytes=64)
             nc.vector.quantize_mx(codes[:].bitcast(E4M3), scales[:], grouped[:].rearrange("p d t -> p (d t)"))
             return codes, scales
 
-        first_xm = quantize_xm(0, interleave_xm(0))
+        def quantize_g(h, grouped):
+            items = slice(h * HALF, (h + 1) * HALF)
+            nc.vector.quantize_mx(
+                g_codes[:, items].bitcast(E5M2), g_scales[:].bitcast(U8)[:, items], grouped[:].rearrange("p i t -> p (i t)")
+            )
 
-        g_grouped = held.tile([P, N, PACK], BF16, name="g_grouped", align_bytes=64)
-        g_dst = g_grouped[:].rearrange("p (e i) t -> p e t i", i=4)
-        g_src = g_rows[:].rearrange("p t (e i) -> p e t i", i=4)
-        nc.vector.tensor_copy(g_dst, g_src)
-        g_codes = held.tile([P, N], U32, name="g_codes", align_bytes=64)
-        g_scales = held.tile([P, N], U8, name="g_scales", align_bytes=64)
-        nc.vector.quantize_mx(g_codes[:].bitcast(E5M2), g_scales[:], g_grouped[:].rearrange("p i t -> p (i t)"))
+        def second_product(k, operand, first, count):
+            codes, scales = operand
+            v = k % (XM_CHUNK // P)
+            cols = slice(v * P, (v + 1) * P)
+            grad = psum_ring.tile([P, N], F32, name="grad")
+            nc.tensor.matmul_mx(
+                grad[:],
+                lhsT=codes[:, cols].bitcast(E4M3), lhsT_scale=scales[:, cols],
+                rhs=g_codes[:].bitcast(E5M2), rhs_scale=g_scales[:].bitcast(U8),
+                start=True, stop=True,
+            )
+            dense = ring.tile([P, count], F32, name="dense")
+            nc.scalar.copy(dense[:], grad[:, first:first + count])
+            return dense
 
-        for c in range(D // XM_CHUNK):
-            codes, scales = first_xm if c == 0 else quantize_xm(c, interleave_xm(c))
-            for v in range(XM_CHUNK // P):
-                k = c * (XM_CHUNK // P) + v
-                cols = slice(v * P, (v + 1) * P)
-                grad = psum_ring.tile([P, N], F32, name="grad")
-                nc.tensor.matmul_mx(
-                    grad[:],
-                    lhsT=codes[:, cols].bitcast(E4M3), lhsT_scale=scales[:, cols],
-                    rhs=g_codes[:].bitcast(E5M2), rhs_scale=g_scales[:],
-                    start=True, stop=True,
-                )
-                dense = ring.tile([P, N], F32, name="dense")
-                nc.scalar.copy(dense[:], grad[:])
-                window = windows[k % WINDOWS]
-                nc.vector.tensor_copy(window[:].indirect(offsets[:]), dense[:])
+        def scatter(k, dense, first, count):
+            window = windows[k % WINDOWS]
+            nc.vector.tensor_copy(window[:].indirect(offsets[:, first // 16:(first + count) // 16]), dense[:])
+            if first + count == N:
                 nc.sync.dma_start(out[k * P:(k + 1) * P, :], window[:])
+
+        yw0 = weigh_targets(0)
+        xm_first = held.tile([P, XM_CHUNK, PACK], BF16, name="xm_first", align_bytes=64)
+        nc.scalar.copy(*interleaved(xm_first, xm_raw[0]))
+        yw1 = weigh_targets(1)
+
+        g_rows0 = held.tile([P, PACK, HALF], BF16, name="g_rows0", tag="xm_codes", align_bytes=64)
+        resid0 = [held.tile([P, HALF], F32, name="resid0_%d" % t) for t in range(PACK)]
+        residual(0, 0, resid0[0][:], yw0)
+        for t in range(1, PACK):
+            residual(0, t, resid0[t][:], yw0)
+            clip(t - 1, g_rows0, resid0[t - 1][:])
+        clip(PACK - 1, g_rows0, resid0[PACK - 1][:])
+        g_grouped0 = held.tile([P, HALF, PACK], BF16, name="g_grouped0", tag="first_half", align_bytes=64)
+        nc.vector.tensor_copy(*interleaved(g_grouped0, g_rows0[:]))
+        operand = quantize_xm(0, xm_first)
+        quantize_g(0, g_grouped0)
+
+        early = [second_product(k, operand, 0, HALF) for k in range(2)]
+
+        resid1 = held.tile([P, PACK, HALF], F32, name="resid1", tag="first_half", align_bytes=64)
+        g_rows1 = held.tile([P, PACK, HALF], BF16, name="g_rows1", tag="xm_grouped", align_bytes=64)
+        for t in range(PACK):
+            residual(1, t, resid1[:, t, :], yw1)
+        for t in range(PACK):
+            clip(t, g_rows1, resid1[:, t, :])
+        g_grouped1 = held.tile([P, HALF, PACK], BF16, name="g_grouped1", align_bytes=64)
+        nc.scalar.copy(*interleaved(g_grouped1, g_rows1[:]))
+
+        scatter(0, early[0], 0, HALF)
+        quantize_g(1, g_grouped1)
+        scatter(1, early[1], 0, HALF)
+        dense = [second_product(k, operand, HALF, HALF) for k in range(2)]
+        first, count = HALF, HALF
+        for c in range(D // XM_CHUNK):
+            if c > 0:
+                dense = [second_product(2 * c + v, operand, 0, N) for v in range(2)]
+                first, count = 0, N
+            if c == 0:
+                operand = quantize_xm(1, interleave_xm(1))
+            scatter(2 * c, dense[0], first, count)
+            if 0 < c < D // XM_CHUNK - 1:
+                operand = quantize_xm(c + 1, interleave_xm(c + 1))
+            scatter(2 * c + 1, dense[1], first, count)

@@ -21,8 +21,10 @@ P = 128
 PACK = 4
 PASSES = D // (P * PACK)
 XM_CHUNK = 256
+XM_CHUNKS = ((0, 256), (256, 256), (512, 512))
 WINDOWS = 3
 HALF = N // 2
+VECTOR_SHARE = 80
 
 
 def tile_attend_ghub_w_kernel(tc, xT, w_words, w_scales, y, wt, xm, offs, out):
@@ -36,15 +38,15 @@ def tile_attend_ghub_w_kernel(tc, xT, w_words, w_scales, y, wt, xm, offs, out):
         offsets = held.tile([P, N // 16], U16, name="offsets")
         nc.sync.dma_start(offsets[:], offs)
 
-        table_words = held.tile([P, T], I32, name="table_words", align_bytes=64)
-        nc.sync.dma_start(table_words[:], w_words[0].rearrange("p t b -> p (t b)").bitcast(I32))
+        w_row = held.tile([P, PACK], F32, name="w_row")
+        nc.sync.dma_start(w_row[:], wt[0].rearrange("(p t) o -> p (t o)", t=PACK))
         table_scales = held.tile([P, T // 4], I32, name="table_scales", tag="scales_then_y", align_bytes=64)
-        nc.vector.memset(table_scales[:], 0)
+        nc.gpsimd.memset(table_scales[:], 0)
         scale_rows = w_scales.bitcast(I32).rearrange("o (q b) t -> b q o t", b=4)
         for b in range(4):
             nc.sync.dma_start(table_scales[b:P:16, :], scale_rows[b])
-        w_row = held.tile([P, PACK], F32, name="w_row")
-        nc.sync.dma_start(w_row[:], wt[0].rearrange("(p t) o -> p (t o)", t=PACK))
+        table_words = held.tile([P, T], I32, name="table_words", tag="words_then_y", align_bytes=64)
+        nc.sync.dma_start(table_words[:], w_words[0].rearrange("p t b -> p (t b)").bitcast(I32))
 
         x_raw = []
         for g in range(PASSES):
@@ -70,31 +72,33 @@ def tile_attend_ghub_w_kernel(tc, xT, w_words, w_scales, y, wt, xm, offs, out):
         nc.scalar.activation(w_lo[:], w_hi[:], ACT.Copy, scale=-1.0)
 
         item_pairs = held.tile([P, N], U32, name="item_pairs", tag="pairs_then_y", align_bytes=64)
-        nc.vector.tensor_copy(item_pairs[:], table_words[:].bitcast(U32).indirect(offsets[:]))
         both_scales = held.tile([P, N], U8, name="both_scales", align_bytes=64)
         nc.vector.tensor_copy(both_scales[:], table_scales[:].bitcast(U8).indirect(offsets[:]))
-        nc.sync.dma_start(moved_scales[0:P - 16, :], both_scales[16:P, :].bitcast(I32))
+        for first, count in ((0, 64), (64, 4), (96, 4)):
+            nc.sync.dma_start(moved_scales[first:first + count, :], both_scales[first + 16:first + 16 + count, :].bitcast(I32))
+        nc.vector.tensor_copy(item_pairs[:], table_words[:].bitcast(U32).indirect(offsets[:]))
         item_scales = [both_scales[:], moved_scales[:].bitcast(U8)]
         item_words = held.tile([P, PASSES, N], U16, name="item_words", align_bytes=64)
         nc.vector.tensor_copy(item_words[:], item_pairs[:].bitcast(U16).rearrange("p (n o) -> p o n", o=PASSES))
 
         y_rows = y[0].rearrange("(p t) i -> p t i", t=PACK)
+        y_raw = []
+        for u, tag in enumerate(("scales_then_y", "words_then_y")):
+            raw = held.tile([P, 2, N], F32, name="y_raw%d" % u, tag=tag, align_bytes=64)
+            nc.sync.dma_start(raw[:], y_rows[:, 2 * u:2 * u + 2, :])
+            y_raw.append(raw)
         xm_rows = xm[0].rearrange("(p t) d -> p t d", t=PACK)
-        y_raw0 = held.tile([P, PACK, HALF], F32, name="y_raw0", tag="scales_then_y", align_bytes=64)
-        nc.sync.dma_start(y_raw0[:], y_rows[:, :, :HALF])
         xm_raw0 = held.tile([P, PACK, XM_CHUNK], F32, name="xm_raw0", tag="pairs_then_y", align_bytes=64)
         nc.sync.dma_start(xm_raw0[:], xm_rows[:, :, :XM_CHUNK])
 
         scores = [psum.tile([P, N], F32, name="scores%d" % t) for t in range(PACK)]
 
-        def interleave_x(g, u, on_vector):
+        def interleave_x(g, u):
             grouped = held.tile([P, 2, P, PACK], BF16, name="x_grouped%d_%d" % (g, u), align_bytes=64)
             src = x_raw[g][:].rearrange("p j (m t) -> p m j t", t=PACK)[:, :, :, 2 * u:2 * u + 2]
             dst = grouped[:].rearrange("p t m j -> p m j t")
-            if on_vector:
-                nc.vector.tensor_copy(dst, src)
-            else:
-                nc.scalar.copy(dst, src)
+            nc.vector.tensor_copy(dst[:, :VECTOR_SHARE], src[:, :VECTOR_SHARE])
+            nc.scalar.copy(dst[:, VECTOR_SHARE:], src[:, VECTOR_SHARE:])
             return grouped
 
         def first_product(g, u, grouped):
@@ -110,31 +114,26 @@ def tile_attend_ghub_w_kernel(tc, xT, w_words, w_scales, y, wt, xm, offs, out):
                     start=(g == 0), stop=(g == PASSES - 1),
                 )
 
-        a0 = interleave_x(0, 0, False)
-        a1 = interleave_x(0, 1, True)
-        first_product(0, 0, a0)
-        first_product(0, 1, a1)
-        rest_raw = held.tile([P, PACK, D], F32, name="rest_raw", tag="x0_then_xm")
-        nc.sync.dma_start(rest_raw[:, :, :HALF], y_rows[:, :, HALF:])
-        for c in range(1, D // XM_CHUNK):
-            chunk = slice(c * XM_CHUNK, (c + 1) * XM_CHUNK)
-            nc.sync.dma_start(rest_raw[:, :, chunk], xm_rows[:, :, chunk])
-        y_raw = [y_raw0[:], rest_raw[:, :, :HALF]]
-        xm_raw = [xm_raw0[:]] + [rest_raw[:, :, c * XM_CHUNK:(c + 1) * XM_CHUNK] for c in range(1, D // XM_CHUNK)]
-        b0 = interleave_x(1, 0, True)
-        b1 = interleave_x(1, 1, False)
-        first_product(1, 0, b0)
-        first_product(1, 1, b1)
+        xm_raw = [xm_raw0]
+        for g in range(PASSES):
+            grouped = [interleave_x(g, u) for u in range(2)]
+            for u in range(2):
+                first_product(g, u, grouped[u])
+            first, width = XM_CHUNKS[g + 1]
+            raw = held.tile([P, PACK, width], F32, name="xm_raw%d" % (g + 1), tag="x%d_then_xm" % g)
+            nc.sync.dma_start(raw[:], xm_rows[:, :, first:first + width])
+            xm_raw.append(raw)
+
+        yw = held.tile([P, PACK, N], F32, name="yw")
 
         def weigh_targets(h):
-            yw = held.tile([P, PACK, HALF], F32, name="yw%d" % h)
+            items = slice(h * HALF, (h + 1) * HALF)
             for t in range(PACK):
-                nc.scalar.activation(yw[:, t, :], y_raw[h][:, t, :], ACT.Copy, scale=w_row[:, t:t + 1])
-            return yw
+                nc.scalar.activation(yw[:, t, items], y_raw[t // 2][:, t % 2, items], ACT.Copy, scale=w_row[:, t:t + 1])
 
-        def residual(h, t, resid, yw):
+        def residual(h, t, resid):
             nc.vector.scalar_tensor_tensor(
-                resid, scores[t][:, h * HALF:(h + 1) * HALF], w_row[:, t:t + 1], yw[:, t, :], ALU.mult, ALU.subtract
+                resid, scores[t][:, h * HALF:(h + 1) * HALF], w_row[:, t:t + 1], yw[:, t, h * HALF:(h + 1) * HALF], ALU.mult, ALU.subtract
             )
 
         def clip(t, g_rows, resid):
@@ -143,14 +142,14 @@ def tile_attend_ghub_w_kernel(tc, xT, w_words, w_scales, y, wt, xm, offs, out):
         def interleaved(grouped, rows):
             return grouped[:].rearrange("p (e i) t -> p e t i", i=4), rows.rearrange("p t (e i) -> p e t i", i=4)
 
-        def interleave_xm(c):
-            grouped = held.tile([P, XM_CHUNK, PACK], BF16, name="xm_grouped%d" % c, tag="xm_grouped", align_bytes=64)
-            nc.scalar.copy(*interleaved(grouped, xm_raw[c]))
+        def interleave_xm(c, tag):
+            grouped = held.tile([P, XM_CHUNKS[c][1], PACK], BF16, name="xm_grouped%d" % c, tag=tag, align_bytes=64)
+            nc.scalar.copy(*interleaved(grouped, xm_raw[c][:]))
             return grouped
 
-        def quantize_xm(c, grouped):
-            codes = held.tile([P, XM_CHUNK], U32, name="xm_codes%d" % c, tag="xm_codes", align_bytes=64)
-            scales = held.tile([P, XM_CHUNK], U8, name="xm_scales%d" % c, tag="xm_scales", align_bytes=64)
+        def quantize_xm(c, grouped, tag):
+            codes = held.tile([P, XM_CHUNKS[c][1]], U32, name="xm_codes%d" % c, tag=tag, align_bytes=64)
+            scales = held.tile([P, XM_CHUNKS[c][1]], U8, name="xm_scales%d" % c, align_bytes=64)
             nc.vector.quantize_mx(codes[:].bitcast(E4M3), scales[:], grouped[:].rearrange("p d t -> p (d t)"))
             return codes, scales
 
@@ -160,9 +159,8 @@ def tile_attend_ghub_w_kernel(tc, xT, w_words, w_scales, y, wt, xm, offs, out):
                 g_codes[:, items].bitcast(E5M2), g_scales[:].bitcast(U8)[:, items], grouped[:].rearrange("p i t -> p (i t)")
             )
 
-        def second_product(k, operand, first, count):
+        def second_product(v, operand, first, count, dense=None):
             codes, scales = operand
-            v = k % (XM_CHUNK // P)
             cols = slice(v * P, (v + 1) * P)
             grad = psum_ring.tile([P, N], F32, name="grad")
             nc.tensor.matmul_mx(
@@ -171,7 +169,8 @@ def tile_attend_ghub_w_kernel(tc, xT, w_words, w_scales, y, wt, xm, offs, out):
                 rhs=g_codes[:].bitcast(E5M2), rhs_scale=g_scales[:].bitcast(U8),
                 start=True, stop=True,
             )
-            dense = ring.tile([P, count], F32, name="dense")
+            if dense is None:
+                dense = ring.tile([P, count], F32, name="dense")
             nc.scalar.copy(dense[:], grad[:, first:first + count])
             return dense
 
@@ -181,46 +180,47 @@ def tile_attend_ghub_w_kernel(tc, xT, w_words, w_scales, y, wt, xm, offs, out):
             if first + count == N:
                 nc.sync.dma_start(out[k * P:(k + 1) * P, :], window[:])
 
-        yw0 = weigh_targets(0)
-        xm_first = held.tile([P, XM_CHUNK, PACK], BF16, name="xm_first", align_bytes=64)
-        nc.scalar.copy(*interleaved(xm_first, xm_raw[0]))
-        yw1 = weigh_targets(1)
+        weigh_targets(0)
+        xm_first = interleave_xm(0, "xm_grouped0")
+        weigh_targets(1)
+        xm_second = interleave_xm(1, "xm_grouped1")
 
         g_rows0 = held.tile([P, PACK, HALF], BF16, name="g_rows0", tag="xm_codes", align_bytes=64)
         resid0 = [held.tile([P, HALF], F32, name="resid0_%d" % t) for t in range(PACK)]
-        residual(0, 0, resid0[0][:], yw0)
+        residual(0, 0, resid0[0][:])
         for t in range(1, PACK):
-            residual(0, t, resid0[t][:], yw0)
+            residual(0, t, resid0[t][:])
             clip(t - 1, g_rows0, resid0[t - 1][:])
         clip(PACK - 1, g_rows0, resid0[PACK - 1][:])
         g_grouped0 = held.tile([P, HALF, PACK], BF16, name="g_grouped0", tag="first_half", align_bytes=64)
         nc.vector.tensor_copy(*interleaved(g_grouped0, g_rows0[:]))
-        operand = quantize_xm(0, xm_first)
+        operand = quantize_xm(0, xm_first, "xm_codes")
         quantize_g(0, g_grouped0)
 
-        early = [second_product(k, operand, 0, HALF) for k in range(2)]
+        early = [second_product(0, operand, 0, HALF)]
 
         resid1 = held.tile([P, PACK, HALF], F32, name="resid1", tag="first_half", align_bytes=64)
-        g_rows1 = held.tile([P, PACK, HALF], BF16, name="g_rows1", tag="xm_grouped", align_bytes=64)
+        g_rows1 = held.tile([P, PACK, HALF], BF16, name="g_rows1", tag="rows1_then_dense", align_bytes=64)
         for t in range(PACK):
-            residual(1, t, resid1[:, t, :], yw1)
+            residual(1, t, resid1[:, t, :])
         for t in range(PACK):
             clip(t, g_rows1, resid1[:, t, :])
         g_grouped1 = held.tile([P, HALF, PACK], BF16, name="g_grouped1", align_bytes=64)
         nc.scalar.copy(*interleaved(g_grouped1, g_rows1[:]))
 
+        dense1 = held.tile([P, HALF], F32, name="dense1", tag="rows1_then_dense", align_bytes=64)
+        early.append(second_product(1, operand, 0, HALF, dense1))
+        second = quantize_xm(1, xm_second, "codes1_then_grouped2")
         scatter(0, early[0], 0, HALF)
         quantize_g(1, g_grouped1)
         scatter(1, early[1], 0, HALF)
         dense = [second_product(k, operand, HALF, HALF) for k in range(2)]
-        first, count = HALF, HALF
-        for c in range(D // XM_CHUNK):
-            if c > 0:
-                dense = [second_product(2 * c + v, operand, 0, N) for v in range(2)]
-                first, count = 0, N
-            if c == 0:
-                operand = quantize_xm(1, interleave_xm(1))
-            scatter(2 * c, dense[0], first, count)
-            if 0 < c < D // XM_CHUNK - 1:
-                operand = quantize_xm(c + 1, interleave_xm(c + 1))
-            scatter(2 * c + 1, dense[1], first, count)
+        scatter(0, dense[0], HALF, HALF)
+        scatter(1, dense[1], HALF, HALF)
+        dense2 = held.tile([P, N], F32, name="dense2", tag="dense2_then_codes2", align_bytes=64)
+        dense = [second_product(0, second, 0, N, dense2), second_product(1, second, 0, N)]
+        scatter(2, dense[0], 0, N)
+        operand = quantize_xm(2, interleave_xm(2, "codes1_then_grouped2"), "dense2_then_codes2")
+        scatter(3, dense[1], 0, N)
+        for v in range(4):
+            scatter(4 + v, second_product(v, operand, 0, N), 0, N)

@@ -25,6 +25,7 @@ XM_CHUNKS = ((0, 256), (256, 256), (512, 512))
 WINDOWS = 3
 HALF = N // 2
 VECTOR_SHARE = 80
+G_SHARE = 40
 
 
 def tile_attend_ghub_w_kernel(tc, xT, w_words, w_scales, y, wt, xm, offs, out):
@@ -40,7 +41,7 @@ def tile_attend_ghub_w_kernel(tc, xT, w_words, w_scales, y, wt, xm, offs, out):
 
         w_row = held.tile([P, PACK], F32, name="w_row")
         nc.sync.dma_start(w_row[:], wt[0].rearrange("(p t) o -> p (t o)", t=PACK))
-        table_scales = held.tile([P, T // 4], I32, name="table_scales", tag="scales_then_y", align_bytes=64)
+        table_scales = held.tile([P, T // 4], I32, name="table_scales", tag="scales_pairs_xm", align_bytes=64)
         nc.gpsimd.memset(table_scales[:], 0)
         scale_rows = w_scales.bitcast(I32).rearrange("o (q b) t -> b q o t", b=4)
         for b in range(4):
@@ -61,7 +62,7 @@ def tile_attend_ghub_w_kernel(tc, xT, w_words, w_scales, y, wt, xm, offs, out):
         nc.vector.memset(g_codes[:, HALF:], 0)
         nc.vector.memset(g_scales[:, HALF // 4:], 0)
         windows = []
-        for k in range(WINDOWS):
+        for k in range(WINDOWS - 1):
             window = held.tile([P, T], F32, name="window%d" % k)
             nc.vector.memset(window[:], 0.0)
             windows.append(window)
@@ -71,7 +72,7 @@ def tile_attend_ghub_w_kernel(tc, xT, w_words, w_scales, y, wt, xm, offs, out):
         nc.scalar.activation(w_hi[:], w_row[:], ACT.Abs)
         nc.scalar.activation(w_lo[:], w_hi[:], ACT.Copy, scale=-1.0)
 
-        item_pairs = held.tile([P, N], U32, name="item_pairs", tag="pairs_then_y", align_bytes=64)
+        item_pairs = held.tile([P, N], U32, name="item_pairs", tag="scales_pairs_xm", align_bytes=64)
         both_scales = held.tile([P, N], U8, name="both_scales", align_bytes=64)
         nc.vector.tensor_copy(both_scales[:], table_scales[:].bitcast(U8).indirect(offsets[:]))
         for first, count in ((0, 64), (64, 4), (96, 4)):
@@ -82,19 +83,17 @@ def tile_attend_ghub_w_kernel(tc, xT, w_words, w_scales, y, wt, xm, offs, out):
         nc.vector.tensor_copy(item_words[:], item_pairs[:].bitcast(U16).rearrange("p (n o) -> p o n", o=PASSES))
 
         y_rows = y[0].rearrange("(p t) i -> p t i", t=PACK)
-        y_raw = []
-        for u, tag in enumerate(("scales_then_y", "words_then_y")):
-            raw = held.tile([P, 2, N], F32, name="y_raw%d" % u, tag=tag, align_bytes=64)
-            nc.sync.dma_start(raw[:], y_rows[:, 2 * u:2 * u + 2, :])
-            y_raw.append(raw)
+        y_raw = held.tile([P, PACK, N], F32, name="y_raw", tag="words_then_y", align_bytes=64)
+        for u in range(2):
+            nc.sync.dma_start(y_raw[:, 2 * u:2 * u + 2, :], y_rows[:, 2 * u:2 * u + 2, :])
         xm_rows = xm[0].rearrange("(p t) d -> p t d", t=PACK)
-        xm_raw0 = held.tile([P, PACK, XM_CHUNK], F32, name="xm_raw0", tag="pairs_then_y", align_bytes=64)
+        xm_raw0 = held.tile([P, PACK, XM_CHUNK], F32, name="xm_raw0", tag="scales_pairs_xm", align_bytes=64)
         nc.sync.dma_start(xm_raw0[:], xm_rows[:, :, :XM_CHUNK])
 
         scores = [psum.tile([P, N], F32, name="scores%d" % t) for t in range(PACK)]
 
         def interleave_x(g, u):
-            grouped = held.tile([P, 2, P, PACK], BF16, name="x_grouped%d_%d" % (g, u), align_bytes=64)
+            grouped = held.tile([P, 2, P, PACK], BF16, name="x_grouped%d_%d" % (g, u), tag="x_grouped%d_%d" % (g, u), align_bytes=64)
             src = x_raw[g][:].rearrange("p j (m t) -> p m j t", t=PACK)[:, :, :, 2 * u:2 * u + 2]
             dst = grouped[:].rearrange("p t m j -> p m j t")
             nc.vector.tensor_copy(dst[:, :VECTOR_SHARE], src[:, :VECTOR_SHARE])
@@ -119,6 +118,9 @@ def tile_attend_ghub_w_kernel(tc, xT, w_words, w_scales, y, wt, xm, offs, out):
             grouped = [interleave_x(g, u) for u in range(2)]
             for u in range(2):
                 first_product(g, u, grouped[u])
+            if g == 0:
+                windows.append(held.tile([P, T], F32, name="window2", tag="x_grouped0_1", align_bytes=64))
+            nc.vector.memset(windows[2][:, g * T // 2:(g + 1) * T // 2], 0.0)
             first, width = XM_CHUNKS[g + 1]
             raw = held.tile([P, PACK, width], F32, name="xm_raw%d" % (g + 1), tag="x%d_then_xm" % g)
             nc.sync.dma_start(raw[:], xm_rows[:, :, first:first + width])
@@ -126,15 +128,11 @@ def tile_attend_ghub_w_kernel(tc, xT, w_words, w_scales, y, wt, xm, offs, out):
 
         yw = held.tile([P, PACK, N], F32, name="yw")
 
-        def weigh_targets(h):
-            items = slice(h * HALF, (h + 1) * HALF)
-            for t in range(PACK):
-                nc.scalar.activation(yw[:, t, items], y_raw[t // 2][:, t % 2, items], ACT.Copy, scale=w_row[:, t:t + 1])
+        def weigh_targets(t, items):
+            nc.scalar.activation(yw[:, t, items], y_raw[:, t, items], ACT.Copy, scale=w_row[:, t:t + 1])
 
-        def residual(h, t, resid):
-            nc.vector.scalar_tensor_tensor(
-                resid, scores[t][:, h * HALF:(h + 1) * HALF], w_row[:, t:t + 1], yw[:, t, h * HALF:(h + 1) * HALF], ALU.mult, ALU.subtract
-            )
+        def residual(t, items, resid):
+            nc.vector.scalar_tensor_tensor(resid, scores[t][:, items], w_row[:, t:t + 1], yw[:, t, items], ALU.mult, ALU.subtract)
 
         def clip(t, g_rows, resid):
             nc.vector.tensor_scalar(g_rows[:, t, :], resid, w_lo[:, t:t + 1], w_hi[:, t:t + 1], ALU.max, ALU.min)
@@ -180,33 +178,40 @@ def tile_attend_ghub_w_kernel(tc, xT, w_words, w_scales, y, wt, xm, offs, out):
             if first + count == N:
                 nc.sync.dma_start(out[k * P:(k + 1) * P, :], window[:])
 
-        weigh_targets(0)
+        first_half, second_half, both = slice(0, HALF), slice(HALF, N), slice(0, N)
+        for t in range(PACK):
+            weigh_targets(t, first_half)
         xm_first = interleave_xm(0, "xm_grouped0")
-        weigh_targets(1)
-        xm_second = interleave_xm(1, "xm_grouped1")
+        for t in range(PACK):
+            weigh_targets(t, second_half)
 
         g_rows0 = held.tile([P, PACK, HALF], BF16, name="g_rows0", tag="xm_codes", align_bytes=64)
         resid0 = [held.tile([P, HALF], F32, name="resid0_%d" % t) for t in range(PACK)]
-        residual(0, 0, resid0[0][:])
+        residual(0, first_half, resid0[0][:])
         for t in range(1, PACK):
-            residual(0, t, resid0[t][:])
+            residual(t, first_half, resid0[t][:])
             clip(t - 1, g_rows0, resid0[t - 1][:])
         clip(PACK - 1, g_rows0, resid0[PACK - 1][:])
-        g_grouped0 = held.tile([P, HALF, PACK], BF16, name="g_grouped0", tag="first_half", align_bytes=64)
-        nc.vector.tensor_copy(*interleaved(g_grouped0, g_rows0[:]))
-        operand = quantize_xm(0, xm_first, "xm_codes")
+        g_grouped0 = held.tile([P, HALF, PACK], BF16, name="g_grouped0", tag="rows1_then_dense", align_bytes=64)
+        dst, src = interleaved(g_grouped0, g_rows0[:])
+        nc.vector.tensor_copy(dst[:, :G_SHARE], src[:, :G_SHARE])
+        nc.scalar.copy(dst[:, G_SHARE:], src[:, G_SHARE:])
+        xm_second = interleave_xm(1, "xm_codes")
+        operand = quantize_xm(0, xm_first, "xm_codes0")
         quantize_g(0, g_grouped0)
 
         early = [second_product(0, operand, 0, HALF)]
 
-        resid1 = held.tile([P, PACK, HALF], F32, name="resid1", tag="first_half", align_bytes=64)
-        g_rows1 = held.tile([P, PACK, HALF], BF16, name="g_rows1", tag="rows1_then_dense", align_bytes=64)
+        resid_free = held.tile([P, N], F32, name="resid_free")
+        late = held.tile([P, 2 * N], F32, name="late", tag="rows1_then_dense", align_bytes=64)
+        resid1 = [resid_free[:, :HALF], resid_free[:, HALF:], late[:, :HALF], late[:, HALF:N]]
+        g_rows1 = late[:, N:].bitcast(BF16).rearrange("p (t i) -> p t i", t=PACK)
         for t in range(PACK):
-            residual(1, t, resid1[:, t, :])
+            residual(t, second_half, resid1[t])
         for t in range(PACK):
-            clip(t, g_rows1, resid1[:, t, :])
+            clip(t, g_rows1, resid1[t])
         g_grouped1 = held.tile([P, HALF, PACK], BF16, name="g_grouped1", align_bytes=64)
-        nc.scalar.copy(*interleaved(g_grouped1, g_rows1[:]))
+        nc.scalar.copy(*interleaved(g_grouped1, g_rows1))
 
         dense1 = held.tile([P, HALF], F32, name="dense1", tag="rows1_then_dense", align_bytes=64)
         early.append(second_product(1, operand, 0, HALF, dense1))

@@ -24,7 +24,7 @@ XM_CHUNK = 256
 XM_CHUNKS = ((0, 256), (256, 256), (512, 512))
 WINDOWS = 3
 HALF = N // 2
-VECTOR_SHARE = 80
+VECTOR_SHARE = 64
 G_SHARE = 40
 
 
@@ -36,24 +36,28 @@ def tile_attend_ghub_w_kernel(tc, xT, w_words, w_scales, y, wt, xm, offs, out):
         psum = ctx.enter_context(tc.psum_pool(name="psum", bufs=1))
         psum_ring = ctx.enter_context(tc.psum_pool(name="psum_ring", bufs=4))
 
+        def load_x(g, h):
+            raw = held.tile([P, 2, R], F32, name="x_raw%d_%d" % (g, h), tag="x%d_%d_then_xm" % (g, h))
+            rows = xT[0, g * 512:(g + 1) * 512, :].rearrange("(p j) r -> p j r", j=PACK)
+            nc.sync.dma_start(raw[:], rows[:, 2 * h:2 * h + 2, :])
+            return raw
+
+        x_raw = {(0, 0): load_x(0, 0)}
         offsets = held.tile([P, N // 16], U16, name="offsets")
         nc.sync.dma_start(offsets[:], offs)
 
         w_row = held.tile([P, PACK], F32, name="w_row")
         nc.sync.dma_start(w_row[:], wt[0].rearrange("(p t) o -> p (t o)", t=PACK))
         table_scales = held.tile([P, T // 4], I32, name="table_scales", tag="scales_pairs_xm", align_bytes=64)
-        nc.gpsimd.memset(table_scales[:], 0)
+        nc.vector.memset(table_scales[:], 0)
         scale_rows = w_scales.bitcast(I32).rearrange("o (q b) t -> b q o t", b=4)
         for b in range(4):
             nc.sync.dma_start(table_scales[b:P:16, :], scale_rows[b])
         table_words = held.tile([P, T], I32, name="table_words", tag="words_then_y", align_bytes=64)
         nc.sync.dma_start(table_words[:], w_words[0].rearrange("p t b -> p (t b)").bitcast(I32))
 
-        x_raw = []
-        for g in range(PASSES):
-            raw = held.tile([P, PACK, R], F32, name="x_raw%d" % g, tag="x%d_then_xm" % g)
-            nc.sync.dma_start(raw[:], xT[0, g * 512:(g + 1) * 512, :].rearrange("(p j) r -> p j r", j=PACK))
-            x_raw.append(raw)
+        for g, h in ((0, 1), (1, 0), (1, 1)):
+            x_raw.setdefault((g, h), load_x(g, h))
 
         moved_scales = held.tile([P, N // 4], I32, name="moved_scales", align_bytes=64)
         nc.vector.memset(moved_scales[:], 0)
@@ -62,7 +66,7 @@ def tile_attend_ghub_w_kernel(tc, xT, w_words, w_scales, y, wt, xm, offs, out):
         nc.vector.memset(g_codes[:, HALF:], 0)
         nc.vector.memset(g_scales[:, HALF // 4:], 0)
         windows = []
-        for k in range(WINDOWS - 1):
+        for k in range(WINDOWS):
             window = held.tile([P, T], F32, name="window%d" % k)
             nc.vector.memset(window[:], 0.0)
             windows.append(window)
@@ -83,22 +87,24 @@ def tile_attend_ghub_w_kernel(tc, xT, w_words, w_scales, y, wt, xm, offs, out):
         nc.vector.tensor_copy(item_words[:], item_pairs[:].bitcast(U16).rearrange("p (n o) -> p o n", o=PASSES))
 
         y_rows = y[0].rearrange("(p t) i -> p t i", t=PACK)
-        y_raw = held.tile([P, PACK, N], F32, name="y_raw", tag="words_then_y", align_bytes=64)
-        for u in range(2):
-            nc.sync.dma_start(y_raw[:, 2 * u:2 * u + 2, :], y_rows[:, 2 * u:2 * u + 2, :])
+        y_raw = held.tile([P, PACK * N], F32, name="y_raw", tag="words_then_y", align_bytes=64)
+        y_wide = y_raw[:, :2 * N].rearrange("p (t i) -> p t i", t=2)
+        y_narrow = [y_raw[:, (2 + h) * N:(3 + h) * N].rearrange("p (t i) -> p t i", t=2) for h in range(2)]
+        nc.sync.dma_start(y_wide, y_rows[:, :2, :])
+        nc.sync.dma_start(y_narrow[0], y_rows[:, 2:, :HALF])
         xm_rows = xm[0].rearrange("(p t) d -> p t d", t=PACK)
         xm_raw0 = held.tile([P, PACK, XM_CHUNK], F32, name="xm_raw0", tag="scales_pairs_xm", align_bytes=64)
         nc.sync.dma_start(xm_raw0[:], xm_rows[:, :, :XM_CHUNK])
+        nc.sync.dma_start(y_narrow[1], y_rows[:, 2:, HALF:])
 
         scores = [psum.tile([P, N], F32, name="scores%d" % t) for t in range(PACK)]
 
-        def interleave_x(g, u):
-            grouped = held.tile([P, 2, P, PACK], BF16, name="x_grouped%d_%d" % (g, u), tag="x_grouped%d_%d" % (g, u), align_bytes=64)
-            src = x_raw[g][:].rearrange("p j (m t) -> p m j t", t=PACK)[:, :, :, 2 * u:2 * u + 2]
-            dst = grouped[:].rearrange("p t m j -> p m j t")
-            nc.vector.tensor_copy(dst[:, :VECTOR_SHARE], src[:, :VECTOR_SHARE])
-            nc.scalar.copy(dst[:, VECTOR_SHARE:], src[:, VECTOR_SHARE:])
-            return grouped
+        x_grouped = [[held.tile([P, 2, P, PACK], BF16, name="x_grouped%d_%d" % (g, u), align_bytes=64) for u in range(2)] for g in range(PASSES)]
+
+        def dealt(g, h, u, columns):
+            src = x_raw[g, h][:].rearrange("p j (m t) -> p m t j", t=PACK)[:, columns, 2 * u:2 * u + 2, :]
+            dst = x_grouped[g][u][:].rearrange("p t m j -> p m t j")[:, columns, :, 2 * h:2 * h + 2]
+            return dst, src
 
         def first_product(g, u, grouped):
             codes = held.tile([P, 2 * P], U32, name="x_codes%d_%d" % (g, u), align_bytes=64)
@@ -113,23 +119,33 @@ def tile_attend_ghub_w_kernel(tc, xT, w_words, w_scales, y, wt, xm, offs, out):
                     start=(g == 0), stop=(g == PASSES - 1),
                 )
 
+        whole = slice(0, P)
+        for h in range(2):
+            for u in range(2):
+                nc.scalar.copy(*dealt(0, h, u, whole))
+        first_product(0, 0, x_grouped[0][0])
+        nc.vector.tensor_copy(*dealt(1, 0, 0, whole))
+        nc.scalar.copy(*dealt(1, 0, 1, whole))
+        first_product(0, 1, x_grouped[0][1])
+        nc.vector.tensor_copy(*dealt(1, 1, 0, whole))
+        nc.vector.tensor_copy(*dealt(1, 1, 1, slice(0, VECTOR_SHARE)))
+        nc.scalar.copy(*dealt(1, 1, 1, slice(VECTOR_SHARE, P)))
+        for u in range(2):
+            first_product(1, u, x_grouped[1][u])
+
         xm_raw = [xm_raw0]
         for g in range(PASSES):
-            grouped = [interleave_x(g, u) for u in range(2)]
-            for u in range(2):
-                first_product(g, u, grouped[u])
-            if g == 0:
-                windows.append(held.tile([P, T], F32, name="window2", tag="x_grouped0_1", align_bytes=64))
-            nc.vector.memset(windows[2][:, g * T // 2:(g + 1) * T // 2], 0.0)
             first, width = XM_CHUNKS[g + 1]
-            raw = held.tile([P, PACK, width], F32, name="xm_raw%d" % (g + 1), tag="x%d_then_xm" % g)
+            raw = held.tile([P, PACK, width], F32, name="xm_raw%d" % (g + 1), tag="x%d_1_then_xm" % g)
             nc.sync.dma_start(raw[:], xm_rows[:, :, first:first + width])
             xm_raw.append(raw)
 
         yw = held.tile([P, PACK, N], F32, name="yw")
 
-        def weigh_targets(t, items):
-            nc.scalar.activation(yw[:, t, items], y_raw[:, t, items], ACT.Copy, scale=w_row[:, t:t + 1])
+        def weigh_targets(t, h):
+            items = slice(h * HALF, (h + 1) * HALF)
+            targets = y_wide[:, t, items] if t < 2 else y_narrow[h][:, t - 2, :]
+            nc.scalar.activation(yw[:, t, items], targets, ACT.Copy, scale=w_row[:, t:t + 1])
 
         def residual(t, items, resid):
             nc.vector.scalar_tensor_tensor(resid, scores[t][:, items], w_row[:, t:t + 1], yw[:, t, items], ALU.mult, ALU.subtract)
@@ -139,6 +155,17 @@ def tile_attend_ghub_w_kernel(tc, xT, w_words, w_scales, y, wt, xm, offs, out):
 
         def interleaved(grouped, rows):
             return grouped[:].rearrange("p (e i) t -> p e t i", i=4), rows.rearrange("p t (e i) -> p e t i", i=4)
+
+        def interleave_block(v):
+            grouped = held.tile([P, P, PACK], BF16, name="block_grouped%d" % v, align_bytes=64)
+            nc.scalar.copy(*interleaved(grouped, xm_raw0[:, :, v * P:(v + 1) * P]))
+            return grouped
+
+        def quantize_block(v, grouped):
+            codes = held.tile([P, P], U32, name="block_codes%d" % v, align_bytes=64)
+            scales = held.tile([P, P], U8, name="block_scales%d" % v, align_bytes=64)
+            nc.vector.quantize_mx(codes[:].bitcast(E4M3), scales[:], grouped[:].rearrange("p d t -> p (d t)"))
+            return codes, scales
 
         def interleave_xm(c, tag):
             grouped = held.tile([P, XM_CHUNKS[c][1], PACK], BF16, name="xm_grouped%d" % c, tag=tag, align_bytes=64)
@@ -180,10 +207,8 @@ def tile_attend_ghub_w_kernel(tc, xT, w_words, w_scales, y, wt, xm, offs, out):
 
         first_half, second_half, both = slice(0, HALF), slice(HALF, N), slice(0, N)
         for t in range(PACK):
-            weigh_targets(t, first_half)
-        xm_first = interleave_xm(0, "xm_grouped0")
-        for t in range(PACK):
-            weigh_targets(t, second_half)
+            weigh_targets(t, 0)
+        block0 = interleave_block(0)
 
         g_rows0 = held.tile([P, PACK, HALF], BF16, name="g_rows0", tag="xm_codes", align_bytes=64)
         resid0 = [held.tile([P, HALF], F32, name="resid0_%d" % t) for t in range(PACK)]
@@ -196,11 +221,15 @@ def tile_attend_ghub_w_kernel(tc, xT, w_words, w_scales, y, wt, xm, offs, out):
         dst, src = interleaved(g_grouped0, g_rows0[:])
         nc.vector.tensor_copy(dst[:, :G_SHARE], src[:, :G_SHARE])
         nc.scalar.copy(dst[:, G_SHARE:], src[:, G_SHARE:])
-        xm_second = interleave_xm(1, "xm_codes")
-        operand = quantize_xm(0, xm_first, "xm_codes0")
+        operands = [quantize_block(0, block0)]
         quantize_g(0, g_grouped0)
+        for t in range(PACK):
+            weigh_targets(t, 1)
+        block1 = interleave_block(1)
 
-        early = [second_product(0, operand, 0, HALF)]
+        early = [second_product(0, operands[0], 0, HALF)]
+        xm_second = interleave_xm(1, "xm_codes")
+        operands.append(quantize_block(1, block1))
 
         resid_free = held.tile([P, N], F32, name="resid_free")
         late = held.tile([P, 2 * N], F32, name="late", tag="rows1_then_dense", align_bytes=64)
@@ -214,12 +243,12 @@ def tile_attend_ghub_w_kernel(tc, xT, w_words, w_scales, y, wt, xm, offs, out):
         nc.scalar.copy(*interleaved(g_grouped1, g_rows1))
 
         dense1 = held.tile([P, HALF], F32, name="dense1", tag="rows1_then_dense", align_bytes=64)
-        early.append(second_product(1, operand, 0, HALF, dense1))
+        early.append(second_product(0, operands[1], 0, HALF, dense1))
         second = quantize_xm(1, xm_second, "codes1_then_grouped2")
         scatter(0, early[0], 0, HALF)
         quantize_g(1, g_grouped1)
         scatter(1, early[1], 0, HALF)
-        dense = [second_product(k, operand, HALF, HALF) for k in range(2)]
+        dense = [second_product(0, operands[k], HALF, HALF) for k in range(2)]
         scatter(0, dense[0], HALF, HALF)
         scatter(1, dense[1], HALF, HALF)
         dense2 = held.tile([P, N], F32, name="dense2", tag="dense2_then_codes2", align_bytes=64)

@@ -22,7 +22,7 @@ PACK = 4
 PASSES = D // (P * PACK)
 XM_CHUNK = 256
 XM_CHUNKS = ((0, 256), (256, 256), (512, 512))
-WINDOWS = 3
+WINDOWS = 4
 HALF = N // 2
 VECTOR_SHARE = 64
 G_SHARE = 40
@@ -32,9 +32,9 @@ def tile_attend_ghub_w_kernel(tc, xT, w_words, w_scales, y, wt, xm, offs, out):
     nc = tc.nc
     with ExitStack() as ctx:
         held = ctx.enter_context(tc.tile_pool(name="held", bufs=1))
-        ring = ctx.enter_context(tc.tile_pool(name="ring", bufs=4))
+        ring = ctx.enter_context(tc.tile_pool(name="ring", bufs=2))
         psum = ctx.enter_context(tc.psum_pool(name="psum", bufs=1))
-        psum_ring = ctx.enter_context(tc.psum_pool(name="psum_ring", bufs=4))
+        psum_ring = ctx.enter_context(tc.psum_pool(name="psum_ring", bufs=2))
 
         def load_x(g, h):
             raw = held.tile([P, 2, R], F32, name="x_raw%d_%d" % (g, h), tag="x%d_%d_then_xm" % (g, h))
@@ -61,10 +61,6 @@ def tile_attend_ghub_w_kernel(tc, xT, w_words, w_scales, y, wt, xm, offs, out):
 
         moved_scales = held.tile([P, N // 4], I32, name="moved_scales", align_bytes=64)
         nc.vector.memset(moved_scales[:], 0)
-        g_codes = held.tile([P, N], I32, name="g_codes", align_bytes=64)
-        g_scales = held.tile([P, N // 4], I32, name="g_scales", align_bytes=64)
-        nc.vector.memset(g_codes[:, HALF:], 0)
-        nc.vector.memset(g_scales[:, HALF // 4:], 0)
         windows = []
         for k in range(WINDOWS):
             window = held.tile([P, T], F32, name="window%d" % k)
@@ -156,105 +152,76 @@ def tile_attend_ghub_w_kernel(tc, xT, w_words, w_scales, y, wt, xm, offs, out):
         def interleaved(grouped, rows):
             return grouped[:].rearrange("p (e i) t -> p e t i", i=4), rows.rearrange("p t (e i) -> p e t i", i=4)
 
-        def interleave_block(v):
-            grouped = held.tile([P, P, PACK], BF16, name="block_grouped%d" % v, align_bytes=64)
-            nc.scalar.copy(*interleaved(grouped, xm_raw0[:, :, v * P:(v + 1) * P]))
+        def interleave_block(k):
+            c = max(c for c in range(len(XM_CHUNKS)) if XM_CHUNKS[c][0] <= k * P)
+            first = k * P - XM_CHUNKS[c][0]
+            grouped = ring.tile([P, P, PACK], BF16, name="block_grouped", align_bytes=64)
+            nc.scalar.copy(*interleaved(grouped, xm_raw[c][:, :, first:first + P]))
             return grouped
 
-        def quantize_block(v, grouped):
-            codes = held.tile([P, P], U32, name="block_codes%d" % v, align_bytes=64)
-            scales = held.tile([P, P], U8, name="block_scales%d" % v, align_bytes=64)
-            nc.vector.quantize_mx(codes[:].bitcast(E4M3), scales[:], grouped[:].rearrange("p d t -> p (d t)"))
-            return codes, scales
-
-        def interleave_xm(c, tag):
-            grouped = held.tile([P, XM_CHUNKS[c][1], PACK], BF16, name="xm_grouped%d" % c, tag=tag, align_bytes=64)
-            nc.scalar.copy(*interleaved(grouped, xm_raw[c][:]))
-            return grouped
-
-        def quantize_xm(c, grouped, tag):
-            codes = held.tile([P, XM_CHUNKS[c][1]], U32, name="xm_codes%d" % c, tag=tag, align_bytes=64)
-            scales = held.tile([P, XM_CHUNKS[c][1]], U8, name="xm_scales%d" % c, align_bytes=64)
+        def quantize_block(grouped):
+            codes = ring.tile([P, P], U32, name="block_codes", bufs=3, align_bytes=64)
+            scales = ring.tile([P, P], U8, name="block_scales", bufs=3, align_bytes=64)
             nc.vector.quantize_mx(codes[:].bitcast(E4M3), scales[:], grouped[:].rearrange("p d t -> p (d t)"))
             return codes, scales
 
         def quantize_g(h, grouped):
-            items = slice(h * HALF, (h + 1) * HALF)
-            nc.vector.quantize_mx(
-                g_codes[:, items].bitcast(E5M2), g_scales[:].bitcast(U8)[:, items], grouped[:].rearrange("p i t -> p (i t)")
-            )
+            codes = held.tile([P, HALF], U32, name="g_codes%d" % h, align_bytes=64)
+            scales = held.tile([P, HALF], U8, name="g_scales%d" % h, align_bytes=64)
+            nc.vector.quantize_mx(codes[:].bitcast(E5M2), scales[:], grouped[:].rearrange("p i t -> p (i t)"))
+            return codes, scales
 
-        def second_product(v, operand, first, count, dense=None):
-            codes, scales = operand
-            cols = slice(v * P, (v + 1) * P)
-            grad = psum_ring.tile([P, N], F32, name="grad")
+        def gradient_rows(h):
+            items = slice(h * HALF, (h + 1) * HALF)
+            g_rows = held.tile([P, PACK, HALF], BF16, name="g_rows%d" % h, align_bytes=64)
+            resid = [held.tile([P, HALF], F32, name="resid%d_%d" % (h, t)) for t in range(PACK)]
+            residual(0, items, resid[0][:])
+            for t in range(1, PACK):
+                residual(t, items, resid[t][:])
+                clip(t - 1, g_rows, resid[t - 1][:])
+            clip(PACK - 1, g_rows, resid[PACK - 1][:])
+            grouped = held.tile([P, HALF, PACK], BF16, name="g_grouped%d" % h, align_bytes=64)
+            return grouped, interleaved(grouped, g_rows[:])
+
+        def place(k, h, block, g_half):
+            grad = psum_ring.tile([P, HALF], F32, name="grad%d" % h)
             nc.tensor.matmul_mx(
                 grad[:],
-                lhsT=codes[:, cols].bitcast(E4M3), lhsT_scale=scales[:, cols],
-                rhs=g_codes[:].bitcast(E5M2), rhs_scale=g_scales[:].bitcast(U8),
+                lhsT=block[0][:].bitcast(E4M3), lhsT_scale=block[1][:],
+                rhs=g_half[0][:].bitcast(E5M2), rhs_scale=g_half[1][:],
                 start=True, stop=True,
             )
-            if dense is None:
-                dense = ring.tile([P, count], F32, name="dense")
-            nc.scalar.copy(dense[:], grad[:, first:first + count])
-            return dense
-
-        def scatter(k, dense, first, count):
+            dense = ring.tile([P, HALF], F32, name="dense%d" % h)
             window = windows[k % WINDOWS]
-            nc.vector.tensor_copy(window[:].indirect(offsets[:, first // 16:(first + count) // 16]), dense[:])
-            if first + count == N:
+            places = window[:].indirect(offsets[:, h * HALF // 16:(h + 1) * HALF // 16])
+            if h == 0:
+                nc.scalar.copy(dense[:], grad[:])
+                nc.scalar.activation(places, dense[:], ACT.Copy)
+            else:
+                nc.vector.tensor_copy(dense[:], grad[:])
+                nc.vector.tensor_copy(places, dense[:])
                 nc.sync.dma_start(out[k * P:(k + 1) * P, :], window[:])
 
-        first_half, second_half, both = slice(0, HALF), slice(HALF, N), slice(0, N)
         for t in range(PACK):
             weigh_targets(t, 0)
-        block0 = interleave_block(0)
-
-        g_rows0 = held.tile([P, PACK, HALF], BF16, name="g_rows0", tag="xm_codes", align_bytes=64)
-        resid0 = [held.tile([P, HALF], F32, name="resid0_%d" % t) for t in range(PACK)]
-        residual(0, first_half, resid0[0][:])
-        for t in range(1, PACK):
-            residual(t, first_half, resid0[t][:])
-            clip(t - 1, g_rows0, resid0[t - 1][:])
-        clip(PACK - 1, g_rows0, resid0[PACK - 1][:])
-        g_grouped0 = held.tile([P, HALF, PACK], BF16, name="g_grouped0", tag="rows1_then_dense", align_bytes=64)
-        dst, src = interleaved(g_grouped0, g_rows0[:])
+        grouped = [interleave_block(0)]
+        g_grouped0, (dst, src) = gradient_rows(0)
         nc.vector.tensor_copy(dst[:, :G_SHARE], src[:, :G_SHARE])
         nc.scalar.copy(dst[:, G_SHARE:], src[:, G_SHARE:])
-        operands = [quantize_block(0, block0)]
-        quantize_g(0, g_grouped0)
+        blocks = [quantize_block(grouped[0])]
+        g_halves = [quantize_g(0, g_grouped0)]
         for t in range(PACK):
             weigh_targets(t, 1)
-        block1 = interleave_block(1)
+        blocks.append(quantize_block(interleave_block(1)))
+        place(0, 0, blocks[0], g_halves[0])
 
-        early = [second_product(0, operands[0], 0, HALF)]
-        xm_second = interleave_xm(1, "xm_codes")
-        operands.append(quantize_block(1, block1))
-
-        resid_free = held.tile([P, N], F32, name="resid_free")
-        late = held.tile([P, 2 * N], F32, name="late", tag="rows1_then_dense", align_bytes=64)
-        resid1 = [resid_free[:, :HALF], resid_free[:, HALF:], late[:, :HALF], late[:, HALF:N]]
-        g_rows1 = late[:, N:].bitcast(BF16).rearrange("p (t i) -> p t i", t=PACK)
-        for t in range(PACK):
-            residual(t, second_half, resid1[t])
-        for t in range(PACK):
-            clip(t, g_rows1, resid1[t])
-        g_grouped1 = held.tile([P, HALF, PACK], BF16, name="g_grouped1", align_bytes=64)
-        nc.scalar.copy(*interleaved(g_grouped1, g_rows1))
-
-        dense1 = held.tile([P, HALF], F32, name="dense1", tag="rows1_then_dense", align_bytes=64)
-        early.append(second_product(0, operands[1], 0, HALF, dense1))
-        second = quantize_xm(1, xm_second, "codes1_then_grouped2")
-        scatter(0, early[0], 0, HALF)
-        quantize_g(1, g_grouped1)
-        scatter(1, early[1], 0, HALF)
-        dense = [second_product(0, operands[k], HALF, HALF) for k in range(2)]
-        scatter(0, dense[0], HALF, HALF)
-        scatter(1, dense[1], HALF, HALF)
-        dense2 = held.tile([P, N], F32, name="dense2", tag="dense2_then_codes2", align_bytes=64)
-        dense = [second_product(0, second, 0, N, dense2), second_product(1, second, 0, N)]
-        scatter(2, dense[0], 0, N)
-        operand = quantize_xm(2, interleave_xm(2, "codes1_then_grouped2"), "dense2_then_codes2")
-        scatter(3, dense[1], 0, N)
-        for v in range(4):
-            scatter(4 + v, second_product(v, operand, 0, N), 0, N)
+        g_grouped1, (dst, src) = gradient_rows(1)
+        nc.vector.tensor_copy(dst, src)
+        g_halves.append(quantize_g(1, g_grouped1))
+        blocks.append(quantize_block(interleave_block(2)))
+        for k in range(D // P):
+            if k + 1 < D // P:
+                place(k + 1, 0, blocks[k + 1], g_halves[0])
+            place(k, 1, blocks[k], g_halves[1])
+            if k + 3 < D // P:
+                blocks.append(quantize_block(interleave_block(k + 3)))

@@ -24,17 +24,19 @@ XM_CHUNK = 256
 XM_CHUNKS = ((0, 256), (256, 256), (512, 512))
 WINDOWS = 4
 HALF = N // 2
-VECTOR_SHARE = 64
-G_SHARE = 40
+EARLY_SLOT = (0, 1, 2, 3, 0, 3, 0, 3)
+LATE_AT = (1024, 3072, 1408, 3072, 1792, 3072, 1792, 3072)
+G_SHARE = 20
+FILLER = 512
 
 
 def tile_attend_ghub_w_kernel(tc, xT, w_words, w_scales, y, wt, xm, offs, out):
     nc = tc.nc
     with ExitStack() as ctx:
         held = ctx.enter_context(tc.tile_pool(name="held", bufs=1))
-        ring = ctx.enter_context(tc.tile_pool(name="ring", bufs=2))
+        stage = ctx.enter_context(tc.tile_pool(name="stage", bufs=1))
+        last_x = ctx.enter_context(tc.tile_pool(name="last_x", bufs=1))
         psum = ctx.enter_context(tc.psum_pool(name="psum", bufs=1))
-        psum_ring = ctx.enter_context(tc.psum_pool(name="psum_ring", bufs=2))
 
         def load_x(g, h):
             raw = held.tile([P, 2, R], F32, name="x_raw%d_%d" % (g, h), tag="x%d_%d_then_xm" % (g, h))
@@ -48,12 +50,12 @@ def tile_attend_ghub_w_kernel(tc, xT, w_words, w_scales, y, wt, xm, offs, out):
 
         w_row = held.tile([P, PACK], F32, name="w_row")
         nc.sync.dma_start(w_row[:], wt[0].rearrange("(p t) o -> p (t o)", t=PACK))
-        table_scales = held.tile([P, T // 4], I32, name="table_scales", tag="scales_pairs_xm", align_bytes=64)
+        table_scales = held.tile([P, T // 4], I32, name="table_scales", tag="scales_then_y", align_bytes=64)
         nc.vector.memset(table_scales[:], 0)
         scale_rows = w_scales.bitcast(I32).rearrange("o (q b) t -> b q o t", b=4)
         for b in range(4):
             nc.sync.dma_start(table_scales[b:P:16, :], scale_rows[b])
-        table_words = held.tile([P, T], I32, name="table_words", tag="words_then_y", align_bytes=64)
+        table_words = held.tile([P, T], I32, name="table_words", tag="words_then_xm", align_bytes=64)
         nc.sync.dma_start(table_words[:], w_words[0].rearrange("p t b -> p (t b)").bitcast(I32))
 
         for g, h in ((0, 1), (1, 0), (1, 1)):
@@ -64,7 +66,7 @@ def tile_attend_ghub_w_kernel(tc, xT, w_words, w_scales, y, wt, xm, offs, out):
         windows = []
         for k in range(WINDOWS):
             window = held.tile([P, T], F32, name="window%d" % k)
-            nc.vector.memset(window[:], 0.0)
+            nc.vector.memset(window[:, :T - FILLER * (k == WINDOWS - 1)], 0.0)
             windows.append(window)
 
         w_hi = held.tile([P, PACK], F32, name="w_hi")
@@ -72,7 +74,7 @@ def tile_attend_ghub_w_kernel(tc, xT, w_words, w_scales, y, wt, xm, offs, out):
         nc.scalar.activation(w_hi[:], w_row[:], ACT.Abs)
         nc.scalar.activation(w_lo[:], w_hi[:], ACT.Copy, scale=-1.0)
 
-        item_pairs = held.tile([P, N], U32, name="item_pairs", tag="scales_pairs_xm", align_bytes=64)
+        item_pairs = held.tile([P, N], U32, name="item_pairs", tag="pairs_then_y", align_bytes=64)
         both_scales = held.tile([P, N], U8, name="both_scales", align_bytes=64)
         nc.vector.tensor_copy(both_scales[:], table_scales[:].bitcast(U8).indirect(offsets[:]))
         for first, count in ((0, 64), (64, 4), (96, 4)):
@@ -81,58 +83,73 @@ def tile_attend_ghub_w_kernel(tc, xT, w_words, w_scales, y, wt, xm, offs, out):
         item_scales = [both_scales[:], moved_scales[:].bitcast(U8)]
         item_words = held.tile([P, PASSES, N], U16, name="item_words", align_bytes=64)
         nc.vector.tensor_copy(item_words[:], item_pairs[:].bitcast(U16).rearrange("p (n o) -> p o n", o=PASSES))
+        nc.vector.memset(windows[-1][:, T - FILLER:], 0.0)
 
         y_rows = y[0].rearrange("(p t) i -> p t i", t=PACK)
-        y_raw = held.tile([P, PACK * N], F32, name="y_raw", tag="words_then_y", align_bytes=64)
-        y_wide = y_raw[:, :2 * N].rearrange("p (t i) -> p t i", t=2)
-        y_narrow = [y_raw[:, (2 + h) * N:(3 + h) * N].rearrange("p (t i) -> p t i", t=2) for h in range(2)]
+        y_early = held.tile([P, 3 * N], F32, name="y_early", tag="scales_then_y", align_bytes=64)
+        y_wide = y_early[:, :2 * N].rearrange("p (t i) -> p t i", t=2)
+        y_narrow = [y_early[:, 2 * N:].rearrange("p (t i) -> p t i", t=2)]
         nc.sync.dma_start(y_wide, y_rows[:, :2, :])
         nc.sync.dma_start(y_narrow[0], y_rows[:, 2:, :HALF])
         xm_rows = xm[0].rearrange("(p t) d -> p t d", t=PACK)
-        xm_raw0 = held.tile([P, PACK, XM_CHUNK], F32, name="xm_raw0", tag="scales_pairs_xm", align_bytes=64)
+        xm_raw0 = held.tile([P, PACK, XM_CHUNK], F32, name="xm_raw0", tag="words_then_xm", align_bytes=64)
         nc.sync.dma_start(xm_raw0[:], xm_rows[:, :, :XM_CHUNK])
-        nc.sync.dma_start(y_narrow[1], y_rows[:, 2:, HALF:])
+        y_late = held.tile([P, 2, HALF], F32, name="y_late", tag="pairs_then_y", align_bytes=64)
+        nc.sync.dma_start(y_late[:], y_rows[:, 2:, HALF:])
+        y_narrow.append(y_late[:])
 
-        scores = [psum.tile([P, N], F32, name="scores%d" % t) for t in range(PACK)]
+        scores = [[psum.tile([P, HALF], F32, name="scores%d_%d" % (h, t), tag="bank%d" % (PACK * h + t)) for t in range(PACK)] for h in range(2)]
 
-        x_grouped = [[held.tile([P, 2, P, PACK], BF16, name="x_grouped%d_%d" % (g, u), align_bytes=64) for u in range(2)] for g in range(PASSES)]
+        x_grouped = [[held.tile([P, 2, P, PACK], BF16, name="x_grouped%d_%d" % (g, u), tag="x_grouped%d_%d" % (g, u), align_bytes=64) for u in range(g, 2)] for g in range(PASSES)]
+        x_grouped[1] = [last_x.tile([P, 2, P, PACK], BF16, name="x_grouped1_0", offset=0, align_bytes=64)] + x_grouped[1]
 
         def dealt(g, h, u, columns):
             src = x_raw[g, h][:].rearrange("p j (m t) -> p m t j", t=PACK)[:, columns, 2 * u:2 * u + 2, :]
             dst = x_grouped[g][u][:].rearrange("p t m j -> p m t j")[:, columns, :, 2 * h:2 * h + 2]
             return dst, src
 
-        def first_product(g, u, grouped):
-            codes = held.tile([P, 2 * P], U32, name="x_codes%d_%d" % (g, u), align_bytes=64)
-            scales = held.tile([P, 2 * P], U8, name="x_scales%d_%d" % (g, u), align_bytes=64)
-            nc.vector.quantize_mx(codes[:].bitcast(E4M3), scales[:], grouped[:].rearrange("p t m j -> p (t m j)"))
-            for v in range(2):
-                cols = slice(v * P, (v + 1) * P)
-                nc.tensor.matmul_mx(
-                    scores[2 * u + v][:],
-                    lhsT=codes[:, cols].bitcast(E4M3), lhsT_scale=scales[:, cols],
-                    rhs=item_words[:, g, :].bitcast(E2M1), rhs_scale=item_scales[g],
-                    start=(g == 0), stop=(g == PASSES - 1),
-                )
+        def quantize_x(g, first, count):
+            u, v = divmod(first, 2)
+            codes = held.tile([P, count * P], U32, name="x_codes%d_%d" % (g, first), align_bytes=64)
+            if (g, first) == (1, 2):
+                scales = last_x.tile([P, count * P], U8, name="x_scales_last", offset=0, align_bytes=64)
+            else:
+                scales = held.tile([P, count * P], U8, name="x_scales%d_%d" % (g, first), align_bytes=64)
+            nc.vector.quantize_mx(codes[:].bitcast(E4M3), scales[:], x_grouped[g][u][:, v:v + count].rearrange("p t m j -> p (t m j)"))
+            return [(codes[:, i * P:(i + 1) * P], scales[:, i * P:(i + 1) * P]) for i in range(count)]
+
+        def first_product(g, t, h):
+            items = slice(h * HALF, (h + 1) * HALF)
+            nc.tensor.matmul_mx(
+                scores[h][t][:],
+                lhsT=x_operands[g][t][0].bitcast(E4M3), lhsT_scale=x_operands[g][t][1],
+                rhs=item_words[:, g, items].bitcast(E2M1), rhs_scale=item_scales[g][:, items],
+                start=(g == 0), stop=(g == PASSES - 1),
+            )
 
         whole = slice(0, P)
         for h in range(2):
             for u in range(2):
                 nc.scalar.copy(*dealt(0, h, u, whole))
-        first_product(0, 0, x_grouped[0][0])
+        x_operands = [quantize_x(0, 0, 2)]
         nc.vector.tensor_copy(*dealt(1, 0, 0, whole))
         nc.scalar.copy(*dealt(1, 0, 1, whole))
-        first_product(0, 1, x_grouped[0][1])
+        x_operands[0].extend(quantize_x(0, 2, 2))
         nc.vector.tensor_copy(*dealt(1, 1, 0, whole))
-        nc.vector.tensor_copy(*dealt(1, 1, 1, slice(0, VECTOR_SHARE)))
-        nc.scalar.copy(*dealt(1, 1, 1, slice(VECTOR_SHARE, P)))
-        for u in range(2):
-            first_product(1, u, x_grouped[1][u])
+        nc.scalar.copy(*dealt(1, 1, 1, whole))
+        x_operands.append(quantize_x(1, 0, 1) + quantize_x(1, 1, 1) + quantize_x(1, 2, 2))
+        for h in range(2):
+            for g in range(PASSES):
+                for t in range(PACK):
+                    first_product(g, t, h)
 
         xm_raw = [xm_raw0]
         for g in range(PASSES):
             first, width = XM_CHUNKS[g + 1]
-            raw = held.tile([P, PACK, width], F32, name="xm_raw%d" % (g + 1), tag="x%d_1_then_xm" % g)
+            if g == 0:
+                raw = held.tile([P, PACK, width], F32, name="xm_raw1", tag="x_grouped0_1", align_bytes=64)
+            else:
+                raw = last_x.tile([P, PACK, width], F32, name="xm_raw2", offset=2 * P, align_bytes=64)
             nc.sync.dma_start(raw[:], xm_rows[:, :, first:first + width])
             xm_raw.append(raw)
 
@@ -143,85 +160,137 @@ def tile_attend_ghub_w_kernel(tc, xT, w_words, w_scales, y, wt, xm, offs, out):
             targets = y_wide[:, t, items] if t < 2 else y_narrow[h][:, t - 2, :]
             nc.scalar.activation(yw[:, t, items], targets, ACT.Copy, scale=w_row[:, t:t + 1])
 
-        def residual(t, items, resid):
-            nc.vector.scalar_tensor_tensor(resid, scores[t][:, items], w_row[:, t:t + 1], yw[:, t, items], ALU.mult, ALU.subtract)
-
-        def clip(t, g_rows, resid):
-            nc.vector.tensor_scalar(g_rows[:, t, :], resid, w_lo[:, t:t + 1], w_hi[:, t:t + 1], ALU.max, ALU.min)
-
         def interleaved(grouped, rows):
             return grouped[:].rearrange("p (e i) t -> p e t i", i=4), rows.rearrange("p t (e i) -> p e t i", i=4)
 
-        def interleave_block(k):
-            c = max(c for c in range(len(XM_CHUNKS)) if XM_CHUNKS[c][0] <= k * P)
+        def block_rows(k, count):
+            c = max(j for j in range(len(XM_CHUNKS)) if XM_CHUNKS[j][0] <= k * P)
             first = k * P - XM_CHUNKS[c][0]
-            grouped = ring.tile([P, P, PACK], BF16, name="block_grouped", align_bytes=64)
-            nc.scalar.copy(*interleaved(grouped, xm_raw[c][:, :, first:first + P]))
+            return xm_raw[c][:, :, first:first + count * P]
+
+        def interleave_blocks(copy, k, count, grouped):
+            copy(*interleaved(grouped, block_rows(k, count)))
             return grouped
 
-        def quantize_block(grouped):
-            codes = ring.tile([P, P], U32, name="block_codes", bufs=3, align_bytes=64)
-            scales = ring.tile([P, P], U8, name="block_scales", bufs=3, align_bytes=64)
+        def held_blocks(k, count, tag):
+            return held.tile([P, count * P, PACK], BF16, name="block_grouped%d" % k, tag=tag, align_bytes=64)
+
+        def quantize_blocks(k, count, grouped, scales=None):
+            codes = held.tile([P, count * P], U32, name="block_codes%d" % k, align_bytes=64)
+            if scales is None:
+                scales = held.tile([P, count * P], U8, name="block_scales%d" % k, align_bytes=64)
             nc.vector.quantize_mx(codes[:].bitcast(E4M3), scales[:], grouped[:].rearrange("p d t -> p (d t)"))
-            return codes, scales
+            return [(codes[:, v * P:(v + 1) * P], scales[:, v * P:(v + 1) * P]) for v in range(count)]
+
+        g_codes = held.tile([P, N], U32, name="g_codes", align_bytes=64)
+        g_scales = held.tile([P, N], U8, name="g_scales", align_bytes=64)
 
         def quantize_g(h, grouped):
-            codes = held.tile([P, HALF], U32, name="g_codes%d" % h, align_bytes=64)
-            scales = held.tile([P, HALF], U8, name="g_scales%d" % h, align_bytes=64)
-            nc.vector.quantize_mx(codes[:].bitcast(E5M2), scales[:], grouped[:].rearrange("p i t -> p (i t)"))
-            return codes, scales
+            items = slice(h * HALF, (h + 1) * HALF)
+            nc.vector.quantize_mx(g_codes[:, items].bitcast(E5M2), g_scales[:, items], grouped[:].rearrange("p i t -> p (i t)"))
 
         def gradient_rows(h):
             items = slice(h * HALF, (h + 1) * HALF)
-            g_rows = held.tile([P, PACK, HALF], BF16, name="g_rows%d" % h, align_bytes=64)
-            resid = [held.tile([P, HALF], F32, name="resid%d_%d" % (h, t)) for t in range(PACK)]
-            residual(0, items, resid[0][:])
-            for t in range(1, PACK):
-                residual(t, items, resid[t][:])
-                clip(t - 1, g_rows, resid[t - 1][:])
-            clip(PACK - 1, g_rows, resid[PACK - 1][:])
-            grouped = held.tile([P, HALF, PACK], BF16, name="g_grouped%d" % h, align_bytes=64)
+            g_rows = held.tile([P, PACK, HALF], BF16, name="g_rows%d" % h, tag="g_rows%d" % h, align_bytes=64)
+            resid = [held.tile([P, HALF], F32, name="resid%d_%d" % (h, t), tag="resid%d" % t) for t in range(PACK)]
+            for t in range(PACK):
+                nc.vector.scalar_tensor_tensor(resid[t][:], scores[h][t][:], w_row[:, t:t + 1], yw[:, t, items], ALU.mult, ALU.subtract)
+            for t in range(PACK):
+                nc.vector.tensor_scalar(g_rows[:, t, :], resid[t][:], w_lo[:, t:t + 1], w_hi[:, t:t + 1], ALU.max, ALU.min)
+            grouped = stage.tile([P, HALF, PACK], BF16, name="g_grouped%d" % h, offset=0, align_bytes=64)
             return grouped, interleaved(grouped, g_rows[:])
 
-        def place(k, h, block, g_half):
-            grad = psum_ring.tile([P, HALF], F32, name="grad%d" % h)
+        def second_product(bank, block, first, count):
+            items = slice(first, first + count)
+            grad = psum.tile([P, count], F32, name="grad", tag="bank%d" % bank)
             nc.tensor.matmul_mx(
                 grad[:],
-                lhsT=block[0][:].bitcast(E4M3), lhsT_scale=block[1][:],
-                rhs=g_half[0][:].bitcast(E5M2), rhs_scale=g_half[1][:],
+                lhsT=block[0].bitcast(E4M3), lhsT_scale=block[1],
+                rhs=g_codes[:, items].bitcast(E5M2), rhs_scale=g_scales[:, items],
                 start=True, stop=True,
             )
-            dense = ring.tile([P, HALF], F32, name="dense%d" % h)
-            window = windows[k % WINDOWS]
-            places = window[:].indirect(offsets[:, h * HALF // 16:(h + 1) * HALF // 16])
+            return grad
+
+        def places(k, h):
+            return windows[k % WINDOWS][:].indirect(offsets[:, h * HALF // 16:(h + 1) * HALF // 16])
+
+        def store(k):
+            nc.sync.dma_start(out[k * P:(k + 1) * P, :], windows[k % WINDOWS][:])
+
+        def half_product(k, h, dense):
+            grad = second_product(PACK * h + k % PACK, blocks[k], h * HALF, HALF)
             if h == 0:
-                nc.scalar.copy(dense[:], grad[:])
-                nc.scalar.activation(places, dense[:], ACT.Copy)
+                nc.scalar.copy(dense, grad[:])
             else:
-                nc.vector.tensor_copy(dense[:], grad[:])
-                nc.vector.tensor_copy(places, dense[:])
-                nc.sync.dma_start(out[k * P:(k + 1) * P, :], window[:])
+                nc.vector.tensor_copy(dense, grad[:])
+            return dense
+
+        def early_half(k):
+            dense = held.tile([P, HALF], F32, name="early%d" % k, tag="early%d" % EARLY_SLOT[k], align_bytes=64)
+            return half_product(k, 0, dense[:])
+
+        def late_half(k):
+            dense = stage.tile([P, HALF], F32, name="late%d" % k, offset=LATE_AT[k], align_bytes=64)
+            return half_product(k, 1, dense[:])
+
+        def scatter_early(k):
+            nc.scalar.activation(places(k, 0), early[k], ACT.Copy)
+
+        def scatter_late(k):
+            nc.vector.tensor_copy(places(k, 1), late[k])
+            store(k)
 
         for t in range(PACK):
             weigh_targets(t, 0)
-        grouped = [interleave_block(0)]
-        g_grouped0, (dst, src) = gradient_rows(0)
-        nc.vector.tensor_copy(dst[:, :G_SHARE], src[:, :G_SHARE])
-        nc.scalar.copy(dst[:, G_SHARE:], src[:, G_SHARE:])
-        blocks = [quantize_block(grouped[0])]
-        g_halves = [quantize_g(0, g_grouped0)]
-        for t in range(PACK):
+        for t in range(2):
             weigh_targets(t, 1)
-        blocks.append(quantize_block(interleave_block(1)))
-        place(0, 0, blocks[0], g_halves[0])
+        grouped = interleave_blocks(nc.scalar.copy, 0, 1, held_blocks(0, 1, "block0"))
+        for t in range(2, PACK):
+            weigh_targets(t, 1)
+        g_grouped0, g_copy0 = gradient_rows(0)
+        nc.vector.tensor_copy(g_copy0[0][:, :G_SHARE], g_copy0[1][:, :G_SHARE])
+        nc.scalar.copy(g_copy0[0][:, G_SHARE:], g_copy0[1][:, G_SHARE:])
+        blocks = quantize_blocks(0, 1, grouped)
+        quantize_g(0, g_grouped0)
+        grouped = interleave_blocks(nc.scalar.copy, 1, 1, held_blocks(1, 1, "g_rows0"))
+        early = [early_half(0)]
+        scatter_early(0)
 
-        g_grouped1, (dst, src) = gradient_rows(1)
-        nc.vector.tensor_copy(dst, src)
-        g_halves.append(quantize_g(1, g_grouped1))
-        blocks.append(quantize_block(interleave_block(2)))
-        for k in range(D // P):
+        g_grouped1, g_copy1 = gradient_rows(1)
+        nc.vector.tensor_copy(*g_copy1)
+        quantize_g(1, g_grouped1)
+        blocks.extend(quantize_blocks(1, 1, grouped))
+        early.append(early_half(1))
+        grouped = interleave_blocks(nc.vector.tensor_copy, 2, 2, held_blocks(2, 2, "g_rows1"))
+        late = [late_half(0)]
+        blocks.extend(quantize_blocks(2, 2, grouped))
+        late.append(late_half(1))
+
+        for k in range(0, PACK, 2):
+            by_scalar = interleave_blocks(nc.scalar.copy, k + 4, 1, held_blocks(k + 4, 1, "early%d" % EARLY_SLOT[k]))
+            scatter_late(k)
+            scales = stage.tile([P, P], U8, name="block_scales%d" % (k + 4), offset=LATE_AT[k] + 256, align_bytes=64)
+            blocks.extend(quantize_blocks(k + 4, 1, by_scalar, scales))
+            by_vector = stage.tile([P, P, PACK], BF16, name="block_grouped%d" % (k + 5), offset=LATE_AT[k] - 768, align_bytes=64)
+            interleave_blocks(nc.vector.tensor_copy, k + 5, 1, by_vector)
+            late.append(late_half(k + 2))
+            blocks.extend(quantize_blocks(k + 5, 1, by_vector))
+            if k == 0:
+                scatter_early(1)
+                early.extend([early_half(2), early_half(3)])
+                scatter_early(2)
+            else:
+                early.append(early_half(4))
+                scatter_early(3)
+                early.append(early_half(5))
+                scatter_early(4)
+            scatter_late(k + 1)
+            late.append(late_half(k + 3))
+        for k in range(PACK, D // P):
+            if k + 2 < D // P:
+                early.append(early_half(k + 2))
             if k + 1 < D // P:
-                place(k + 1, 0, blocks[k + 1], g_halves[0])
-            place(k, 1, blocks[k], g_halves[1])
-            if k + 3 < D // P:
-                blocks.append(quantize_block(interleave_block(k + 3)))
+                scatter_early(k + 1)
+            scatter_late(k)
+            if k + 2 < D // P:
+                late.append(late_half(k + 2))

@@ -26,7 +26,7 @@ WINDOWS = 4
 HALF = N // 2
 EARLY_SLOT = (0, 1, 2, 3, 0, 3, 0, 3)
 LATE_AT = (1024, 3072, 1408, 3072, 1792, 3072, 1792, 3072)
-G_SHARE = 20
+G_SHARE = 32
 FILLER = 512
 
 
@@ -66,7 +66,7 @@ def tile_attend_ghub_w_kernel(tc, xT, w_words, w_scales, y, wt, xm, offs, out):
         windows = []
         for k in range(WINDOWS):
             window = held.tile([P, T], F32, name="window%d" % k)
-            nc.vector.memset(window[:, :T - FILLER * (k == WINDOWS - 1)], 0.0)
+            nc.vector.memset(window[:, :T - FILLER * (k == WINDOWS - 1)].bitcast(I32), 0)
             windows.append(window)
 
         w_hi = held.tile([P, PACK], F32, name="w_hi")
@@ -83,7 +83,7 @@ def tile_attend_ghub_w_kernel(tc, xT, w_words, w_scales, y, wt, xm, offs, out):
         item_scales = [both_scales[:], moved_scales[:].bitcast(U8)]
         item_words = held.tile([P, PASSES, N], U16, name="item_words", align_bytes=64)
         nc.vector.tensor_copy(item_words[:], item_pairs[:].bitcast(U16).rearrange("p (n o) -> p o n", o=PASSES))
-        nc.vector.memset(windows[-1][:, T - FILLER:], 0.0)
+        nc.vector.memset(windows[-1][:, T - FILLER:].bitcast(I32), 0)
 
         y_rows = y[0].rearrange("(p t) i -> p t i", t=PACK)
         y_early = held.tile([P, 3 * N], F32, name="y_early", tag="scales_then_y", align_bytes=64)

@@ -20,185 +20,181 @@ ACT = mybir.ActivationFunctionType
 P = 128
 PACK = 4
 PASSES = D // (P * PACK)
-XM_CHUNK = 256
-XM_CHUNKS = ((0, 256), (256, 256), (512, 512))
-WINDOWS = 4
+BLOCKS = D // P
 HALF = N // 2
-EARLY_SLOT = (0, 1, 2, 3, 0, 3, 0, 3)
-LATE_AT = (1024, 3072, 1408, 3072, 1792, 3072, 1792, 3072)
-G_SHARE = 32
-FILLER = 512
+WINDOWS = 4
+G_SHARE = 48
+EARLY_AT = (0, 1024, 3072, 1024, 4032, 1088, 4032, 1088)
+LATE_AT = (1024, 3072, 1984, 4032, 1920, 3072, 4992, 1920)
+XM_CHUNKS = ((0, 256), (256, 256), (512, 512))
 
 
 def tile_attend_ghub_w_kernel(tc, xT, w_words, w_scales, y, wt, xm, offs, out):
     nc = tc.nc
     with ExitStack() as ctx:
         held = ctx.enter_context(tc.tile_pool(name="held", bufs=1))
-        stage = ctx.enter_context(tc.tile_pool(name="stage", bufs=1))
-        last_x = ctx.enter_context(tc.tile_pool(name="last_x", bufs=1))
+        words_then_xm = ctx.enter_context(tc.tile_pool(name="words_then_xm", bufs=1))
+        rows_then_xm = ctx.enter_context(tc.tile_pool(name="rows_then_xm", bufs=1))
+        scalar_stage = ctx.enter_context(tc.tile_pool(name="scalar_stage", bufs=1))
+        vector_stage = ctx.enter_context(tc.tile_pool(name="vector_stage", bufs=1))
         psum = ctx.enter_context(tc.psum_pool(name="psum", bufs=1))
 
-        def load_x(g, h):
-            raw = held.tile([P, 2, R], F32, name="x_raw%d_%d" % (g, h), tag="x%d_%d_then_xm" % (g, h))
+        def load_x(g, first, count):
+            raw = held.tile([P, count, R], F32, name="x_raw%d_%d" % (g, first), tag="x_raw%d_%d" % (g, first))
             rows = xT[0, g * 512:(g + 1) * 512, :].rearrange("(p j) r -> p j r", j=PACK)
-            nc.sync.dma_start(raw[:], rows[:, 2 * h:2 * h + 2, :])
+            nc.sync.dma_start(raw[:], rows[:, first:first + count, :])
             return raw
 
-        x_raw = {(0, 0): load_x(0, 0)}
+        x_raw = [load_x(0, 0, 2)]
         offsets = held.tile([P, N // 16], U16, name="offsets")
         nc.sync.dma_start(offsets[:], offs)
-
-        w_row = held.tile([P, PACK], F32, name="w_row")
-        nc.sync.dma_start(w_row[:], wt[0].rearrange("(p t) o -> p (t o)", t=PACK))
         table_scales = held.tile([P, T // 4], I32, name="table_scales", tag="scales_then_y", align_bytes=64)
         nc.vector.memset(table_scales[:], 0)
         scale_rows = w_scales.bitcast(I32).rearrange("o (q b) t -> b q o t", b=4)
         for b in range(4):
             nc.sync.dma_start(table_scales[b:P:16, :], scale_rows[b])
-        table_words = held.tile([P, T], I32, name="table_words", tag="words_then_xm", align_bytes=64)
+        table_words = words_then_xm.tile([P, T], I32, name="table_words", offset=0, align_bytes=64)
         nc.sync.dma_start(table_words[:], w_words[0].rearrange("p t b -> p (t b)").bitcast(I32))
+        x_raw.extend([load_x(0, 2, 2), load_x(1, 0, 2), load_x(1, 2, 2)])
 
-        for g, h in ((0, 1), (1, 0), (1, 1)):
-            x_raw.setdefault((g, h), load_x(g, h))
+        w_row = held.tile([P, PACK], F32, name="w_row")
+        nc.sync.dma_start(w_row[:], wt[0].rearrange("(p t) o -> p (t o)", t=PACK))
 
         moved_scales = held.tile([P, N // 4], I32, name="moved_scales", align_bytes=64)
         nc.vector.memset(moved_scales[:], 0)
-        windows = []
-        for k in range(WINDOWS):
-            window = held.tile([P, T], F32, name="window%d" % k)
-            nc.vector.memset(window[:, :T - FILLER * (k == WINDOWS - 1)].bitcast(I32), 0)
-            windows.append(window)
+        windows = [held.tile([P, T], F32, name="window%d" % k) for k in range(WINDOWS)]
+
+        def zero(k, first, count):
+            nc.vector.memset(windows[k][:, first:first + count].bitcast(I32), 0)
+
+        for k in range(WINDOWS - 1):
+            zero(k, 0, T)
+
+        x_grouped = [[held.tile([P, 2, P, PACK], BF16, name="x_grouped%d_%d" % (g, u), align_bytes=64) for u in range(2)] for g in range(PASSES)]
+
+        def deal(copy, raw, g, u, first):
+            src = raw[:].rearrange("p j (m t) -> p m j t", t=PACK)[:, :, :, 2 * u:2 * u + 2]
+            copy(x_grouped[g][u][:].rearrange("p t m j -> p m j t")[:, :, first:first + src.shape[2]], src)
+
+        def quantize(name, grouped, scales=None):
+            width = grouped.shape[1] // PACK
+            codes = held.tile([P, width], U32, name=name + "_codes", align_bytes=64)
+            if scales is None:
+                scales = held.tile([P, width], U8, name=name + "_scales", align_bytes=64)
+            nc.vector.quantize_mx(codes[:].bitcast(E4M3), scales[:, :], grouped)
+            return [(codes[:, c:c + P], scales[:, c:c + P]) for c in range(0, width, P)]
+
+        def quantize_x(g, first, count):
+            u, v = divmod(first, 2)
+            return quantize("x%d_%d" % (g, first), x_grouped[g][u][:, v:v + count].rearrange("p t m j -> p (t m j)"))
+
+        def entries(first, count):
+            return offsets[:, first // 16:(first + count) // 16]
+
+        for u in range(2):
+            deal(nc.scalar.copy, x_raw[0], 0, u, 0)
+        for u in range(2):
+            deal(nc.scalar.copy, x_raw[1], 0, u, 2)
+
+        both_scales = held.tile([P, N], U8, name="both_scales", align_bytes=64)
+        nc.vector.tensor_copy(both_scales[:], table_scales[:].bitcast(U8).indirect(offsets[:]))
+        for first, count in ((0, 64), (64, 4), (96, 4)):
+            nc.sync.dma_start(moved_scales[first:first + count, :], both_scales[first + 16:first + 16 + count, :].bitcast(I32))
+        item_scales = [both_scales[:], moved_scales[:].bitcast(U8)]
+
+        targets = held.tile([P, PACK, N], F32, name="targets", tag="scales_then_y", align_bytes=64)
+        y_rows = y[0].rearrange("(p t) i -> p t i", t=PACK)
+        nc.sync.dma_start(targets[:, :2, :], y_rows[:, :2, :])
+        nc.sync.dma_start(targets[:, 2:, :HALF], y_rows[:, 2:, :HALF])
+
+        def gather_pairs(h):
+            pairs = held.tile([P, HALF], U32, name="item_pairs%d" % h, tag="item_pairs%d" % h, align_bytes=64)
+            nc.vector.tensor_copy(pairs[:], table_words[:].bitcast(U32).indirect(entries(h * HALF, HALF)))
+            return pairs
+
+        def part_pairs(h, pairs):
+            words = held.tile([P, PASSES, HALF], U16, name="item_words%d" % h, align_bytes=64)
+            nc.vector.tensor_copy(words[:], pairs[:].bitcast(U16).rearrange("p (n o) -> p o n", o=PASSES))
+            return words
+
+        zero(WINDOWS - 1, 0, T // 2)
+        pairs = [gather_pairs(h) for h in range(2)]
+        item_words = [part_pairs(h, pairs[h]) for h in range(2)]
+        x_operands = [quantize_x(0, 0, 2)]
+        zero(WINDOWS - 1, T // 2, T // 2)
+        x_operands[0].extend(quantize_x(0, 2, 2))
+
+        xm_rows = xm[0].rearrange("(p t) d -> p t d", t=PACK)
+        xm_raw = []
+        for c, (first, width) in enumerate(XM_CHUNKS):
+            if c < 2:
+                raw = words_then_xm.tile([P, PACK, width], F32, name="xm_raw%d" % c, offset=first * PACK * 4, align_bytes=64)
+            else:
+                raw = held.tile([P, PACK, width], F32, name="xm_raw%d" % c, tag="x_raw1_2")
+            xm_raw.append(raw)
+
+        def load_xm(c):
+            first, width = XM_CHUNKS[c]
+            nc.sync.dma_start(xm_raw[c][:], xm_rows[:, :, first:first + width])
+
+        load_xm(0)
+        late_targets = held.tile([P, 2, HALF], F32, name="late_targets", tag="item_pairs1", align_bytes=64)
+        nc.sync.dma_start(late_targets[:], y_rows[:, 2:, HALF:])
+        load_xm(1)
+
+        scores0 = [psum.tile([P, HALF], F32, name="scores0_%d" % t, tag="bank%d" % t) for t in range(PACK)]
+        scores1 = [psum.tile([P, 2, HALF], F32, name="scores1_%d" % u, tag="bank%d" % (PACK, 0)[u]) for u in range(2)]
+
+        def first_product(g, h, t, sums, opens, closes):
+            nc.tensor.matmul_mx(
+                sums,
+                lhsT=x_operands[g][t][0].bitcast(E4M3), lhsT_scale=x_operands[g][t][1],
+                rhs=item_words[h][:, g, :].bitcast(E2M1), rhs_scale=item_scales[g][:, h * HALF:(h + 1) * HALF],
+                start=opens, stop=closes,
+            )
+
+        for piece in range(2):
+            deal(nc.vector.tensor_copy, x_raw[2 + piece], 1, 0, 2 * piece)
+            deal(nc.scalar.copy, x_raw[2 + piece], 1, 1, 2 * piece)
+        x_operands.append(quantize_x(1, 0, 1) + quantize_x(1, 1, 1) + quantize_x(1, 2, 2))
+        for g in range(PASSES):
+            for t in range(PACK):
+                first_product(g, 0, t, scores0[t][:], g == 0, g == PASSES - 1)
+        for u in range(2):
+            for g in range(PASSES):
+                for v in range(2):
+                    first_product(g, 1, 2 * u + v, scores1[u][:, v, :], (g, v) == (0, 0), (g, v) == (PASSES - 1, 1))
+        load_xm(2)
 
         w_hi = held.tile([P, PACK], F32, name="w_hi")
         w_lo = held.tile([P, PACK], F32, name="w_lo")
         nc.scalar.activation(w_hi[:], w_row[:], ACT.Abs)
         nc.scalar.activation(w_lo[:], w_hi[:], ACT.Copy, scale=-1.0)
 
-        item_pairs = held.tile([P, N], U32, name="item_pairs", tag="pairs_then_y", align_bytes=64)
-        both_scales = held.tile([P, N], U8, name="both_scales", align_bytes=64)
-        nc.vector.tensor_copy(both_scales[:], table_scales[:].bitcast(U8).indirect(offsets[:]))
-        for first, count in ((0, 64), (64, 4), (96, 4)):
-            nc.sync.dma_start(moved_scales[first:first + count, :], both_scales[first + 16:first + 16 + count, :].bitcast(I32))
-        nc.vector.tensor_copy(item_pairs[:], table_words[:].bitcast(U32).indirect(offsets[:]))
-        item_scales = [both_scales[:], moved_scales[:].bitcast(U8)]
-        item_words = held.tile([P, PASSES, N], U16, name="item_words", align_bytes=64)
-        nc.vector.tensor_copy(item_words[:], item_pairs[:].bitcast(U16).rearrange("p (n o) -> p o n", o=PASSES))
-        nc.vector.memset(windows[-1][:, T - FILLER:].bitcast(I32), 0)
+        weighted = []
+        for t in range(PACK):
+            yw = held.tile([P, HALF], F32, name="yw%d" % t, align_bytes=64)
+            nc.scalar.activation(yw[:], targets[:, t, :HALF], ACT.Copy, scale=w_row[:, t:t + 1])
+            weighted.append(yw)
 
-        y_rows = y[0].rearrange("(p t) i -> p t i", t=PACK)
-        y_early = held.tile([P, 3 * N], F32, name="y_early", tag="scales_then_y", align_bytes=64)
-        y_wide = y_early[:, :2 * N].rearrange("p (t i) -> p t i", t=2)
-        y_narrow = [y_early[:, 2 * N:].rearrange("p (t i) -> p t i", t=2)]
-        nc.sync.dma_start(y_wide, y_rows[:, :2, :])
-        nc.sync.dma_start(y_narrow[0], y_rows[:, 2:, :HALF])
-        xm_rows = xm[0].rearrange("(p t) d -> p t d", t=PACK)
-        xm_raw0 = held.tile([P, PACK, XM_CHUNK], F32, name="xm_raw0", tag="words_then_xm", align_bytes=64)
-        nc.sync.dma_start(xm_raw0[:], xm_rows[:, :, :XM_CHUNK])
-        y_late = held.tile([P, 2, HALF], F32, name="y_late", tag="pairs_then_y", align_bytes=64)
-        nc.sync.dma_start(y_late[:], y_rows[:, 2:, HALF:])
-        y_narrow.append(y_late[:])
-
-        scores = [[psum.tile([P, HALF], F32, name="scores%d_%d" % (h, t), tag="bank%d" % (PACK * h + t)) for t in range(PACK)] for h in range(2)]
-
-        x_grouped = [[held.tile([P, 2, P, PACK], BF16, name="x_grouped%d_%d" % (g, u), tag="x_grouped%d_%d" % (g, u), align_bytes=64) for u in range(g, 2)] for g in range(PASSES)]
-        x_grouped[1] = [last_x.tile([P, 2, P, PACK], BF16, name="x_grouped1_0", offset=0, align_bytes=64)] + x_grouped[1]
-
-        def dealt(g, h, u, columns):
-            src = x_raw[g, h][:].rearrange("p j (m t) -> p m t j", t=PACK)[:, columns, 2 * u:2 * u + 2, :]
-            dst = x_grouped[g][u][:].rearrange("p t m j -> p m t j")[:, columns, :, 2 * h:2 * h + 2]
-            return dst, src
-
-        def quantize_x(g, first, count):
-            u, v = divmod(first, 2)
-            codes = held.tile([P, count * P], U32, name="x_codes%d_%d" % (g, first), align_bytes=64)
-            if (g, first) == (1, 2):
-                scales = last_x.tile([P, count * P], U8, name="x_scales_last", offset=0, align_bytes=64)
-            else:
-                scales = held.tile([P, count * P], U8, name="x_scales%d_%d" % (g, first), align_bytes=64)
-            nc.vector.quantize_mx(codes[:].bitcast(E4M3), scales[:], x_grouped[g][u][:, v:v + count].rearrange("p t m j -> p (t m j)"))
-            return [(codes[:, i * P:(i + 1) * P], scales[:, i * P:(i + 1) * P]) for i in range(count)]
-
-        def first_product(g, t, h):
-            items = slice(h * HALF, (h + 1) * HALF)
-            nc.tensor.matmul_mx(
-                scores[h][t][:],
-                lhsT=x_operands[g][t][0].bitcast(E4M3), lhsT_scale=x_operands[g][t][1],
-                rhs=item_words[:, g, items].bitcast(E2M1), rhs_scale=item_scales[g][:, items],
-                start=(g == 0), stop=(g == PASSES - 1),
-            )
-
-        whole = slice(0, P)
-        for h in range(2):
-            for u in range(2):
-                nc.scalar.copy(*dealt(0, h, u, whole))
-        x_operands = [quantize_x(0, 0, 2)]
-        nc.vector.tensor_copy(*dealt(1, 0, 0, whole))
-        nc.scalar.copy(*dealt(1, 0, 1, whole))
-        x_operands[0].extend(quantize_x(0, 2, 2))
-        nc.vector.tensor_copy(*dealt(1, 1, 0, whole))
-        nc.scalar.copy(*dealt(1, 1, 1, whole))
-        x_operands.append(quantize_x(1, 0, 1) + quantize_x(1, 1, 1) + quantize_x(1, 2, 2))
-        for h in range(2):
-            for g in range(PASSES):
-                for t in range(PACK):
-                    first_product(g, t, h)
-
-        xm_raw = [xm_raw0]
-        for g in range(PASSES):
-            first, width = XM_CHUNKS[g + 1]
-            if g == 0:
-                raw = held.tile([P, PACK, width], F32, name="xm_raw1", tag="x_grouped0_1", align_bytes=64)
-            else:
-                raw = last_x.tile([P, PACK, width], F32, name="xm_raw2", offset=2 * P, align_bytes=64)
-            nc.sync.dma_start(raw[:], xm_rows[:, :, first:first + width])
-            xm_raw.append(raw)
-
-        yw = held.tile([P, PACK, N], F32, name="yw")
-
-        def weigh_targets(t, h):
-            items = slice(h * HALF, (h + 1) * HALF)
-            targets = y_wide[:, t, items] if t < 2 else y_narrow[h][:, t - 2, :]
-            nc.scalar.activation(yw[:, t, items], targets, ACT.Copy, scale=w_row[:, t:t + 1])
-
-        def interleaved(grouped, rows):
-            return grouped[:].rearrange("p (e i) t -> p e t i", i=4), rows.rearrange("p t (e i) -> p e t i", i=4)
-
-        def block_rows(k, count):
-            c = max(j for j in range(len(XM_CHUNKS)) if XM_CHUNKS[j][0] <= k * P)
-            first = k * P - XM_CHUNKS[c][0]
-            return xm_raw[c][:, :, first:first + count * P]
-
-        def interleave_blocks(copy, k, count, grouped):
-            copy(*interleaved(grouped, block_rows(k, count)))
+        def interleave(copy, grouped, rows):
+            copy(grouped.rearrange("p (e i) t -> p e t i", i=4), rows.rearrange("p t (e i) -> p e t i", i=4))
             return grouped
 
-        def held_blocks(k, count, tag):
-            return held.tile([P, count * P, PACK], BF16, name="block_grouped%d" % k, tag=tag, align_bytes=64)
+        def interleave_block(copy, k, grouped):
+            c = max(j for j in range(len(XM_CHUNKS)) if XM_CHUNKS[j][0] <= k * P)
+            first = k * P - XM_CHUNKS[c][0]
+            return interleave(copy, grouped, xm_raw[c][:, :, first:first + grouped.shape[1]])
 
-        def quantize_blocks(k, count, grouped, scales=None):
-            codes = held.tile([P, count * P], U32, name="block_codes%d" % k, align_bytes=64)
-            if scales is None:
-                scales = held.tile([P, count * P], U8, name="block_scales%d" % k, align_bytes=64)
-            nc.vector.quantize_mx(codes[:].bitcast(E4M3), scales[:], grouped[:].rearrange("p d t -> p (d t)"))
-            return [(codes[:, v * P:(v + 1) * P], scales[:, v * P:(v + 1) * P]) for v in range(count)]
+        def quantize_blocks(k, grouped, scales=None):
+            return quantize("block%d" % k, grouped.rearrange("p d t -> p (d t)"), scales)
 
         g_codes = held.tile([P, N], U32, name="g_codes", align_bytes=64)
         g_scales = held.tile([P, N], U8, name="g_scales", align_bytes=64)
 
-        def quantize_g(h, grouped):
-            items = slice(h * HALF, (h + 1) * HALF)
-            nc.vector.quantize_mx(g_codes[:, items].bitcast(E5M2), g_scales[:, items], grouped[:].rearrange("p i t -> p (i t)"))
-
-        def gradient_rows(h):
-            items = slice(h * HALF, (h + 1) * HALF)
-            g_rows = held.tile([P, PACK, HALF], BF16, name="g_rows%d" % h, tag="g_rows%d" % h, align_bytes=64)
-            resid = [held.tile([P, HALF], F32, name="resid%d_%d" % (h, t), tag="resid%d" % t) for t in range(PACK)]
-            for t in range(PACK):
-                nc.vector.scalar_tensor_tensor(resid[t][:], scores[h][t][:], w_row[:, t:t + 1], yw[:, t, items], ALU.mult, ALU.subtract)
-            for t in range(PACK):
-                nc.vector.tensor_scalar(g_rows[:, t, :], resid[t][:], w_lo[:, t:t + 1], w_hi[:, t:t + 1], ALU.max, ALU.min)
-            grouped = stage.tile([P, HALF, PACK], BF16, name="g_grouped%d" % h, offset=0, align_bytes=64)
-            return grouped, interleaved(grouped, g_rows[:])
+        def quantize_g(first, grouped):
+            items = slice(first, first + grouped.shape[1])
+            nc.vector.quantize_mx(g_codes[:, items].bitcast(E5M2), g_scales[:, items], grouped.rearrange("p i t -> p (i t)"))
 
         def second_product(bank, block, first, count):
             items = slice(first, first + count)
@@ -212,85 +208,109 @@ def tile_attend_ghub_w_kernel(tc, xT, w_words, w_scales, y, wt, xm, offs, out):
             return grad
 
         def places(k, h):
-            return windows[k % WINDOWS][:].indirect(offsets[:, h * HALF // 16:(h + 1) * HALF // 16])
-
-        def store(k):
-            nc.sync.dma_start(out[k * P:(k + 1) * P, :], windows[k % WINDOWS][:])
-
-        def half_product(k, h, dense):
-            grad = second_product(PACK * h + k % PACK, blocks[k], h * HALF, HALF)
-            if h == 0:
-                nc.scalar.copy(dense, grad[:])
-            else:
-                nc.vector.tensor_copy(dense, grad[:])
-            return dense
+            return windows[k % WINDOWS][:].indirect(entries(h * HALF, HALF))
 
         def early_half(k):
-            dense = held.tile([P, HALF], F32, name="early%d" % k, tag="early%d" % EARLY_SLOT[k], align_bytes=64)
-            return half_product(k, 0, dense[:])
+            grad = second_product(2 + k % 2, blocks[k], 0, HALF)
+            dense = scalar_stage.tile([P, HALF], F32, name="early%d" % k, offset=EARLY_AT[k], align_bytes=64)
+            nc.scalar.copy(dense[:], grad[:])
+            return dense
 
         def late_half(k):
-            dense = stage.tile([P, HALF], F32, name="late%d" % k, offset=LATE_AT[k], align_bytes=64)
-            return half_product(k, 1, dense[:])
+            grad = second_product(5 + k % 3, blocks[k], HALF, HALF)
+            dense = vector_stage.tile([P, HALF], F32, name="late%d" % k, offset=LATE_AT[k], align_bytes=64)
+            nc.vector.tensor_copy(dense[:], grad[:])
+            return dense
 
         def scatter_early(k):
-            nc.scalar.activation(places(k, 0), early[k], ACT.Copy)
+            nc.scalar.activation(places(k, 0), early[k][:], ACT.Copy)
 
         def scatter_late(k):
-            nc.vector.tensor_copy(places(k, 1), late[k])
-            store(k)
+            nc.vector.tensor_copy(places(k, 1), late[k][:])
+            nc.sync.dma_start(out[k * P:(k + 1) * P, :], windows[k % WINDOWS][:])
 
+        resid0 = held.tile([P, PACK, HALF], F32, name="resid0", tag="resid")
         for t in range(PACK):
-            weigh_targets(t, 0)
-        for t in range(2):
-            weigh_targets(t, 1)
-        grouped = interleave_blocks(nc.scalar.copy, 0, 1, held_blocks(0, 1, "block0"))
-        for t in range(2, PACK):
-            weigh_targets(t, 1)
-        g_grouped0, g_copy0 = gradient_rows(0)
-        nc.vector.tensor_copy(g_copy0[0][:, :G_SHARE], g_copy0[1][:, :G_SHARE])
-        nc.scalar.copy(g_copy0[0][:, G_SHARE:], g_copy0[1][:, G_SHARE:])
-        blocks = quantize_blocks(0, 1, grouped)
-        quantize_g(0, g_grouped0)
-        grouped = interleave_blocks(nc.scalar.copy, 1, 1, held_blocks(1, 1, "g_rows0"))
+            nc.vector.scalar_tensor_tensor(resid0[:, t, :], scores0[t][:], w_row[:, t:t + 1], weighted[t][:], ALU.mult, ALU.subtract)
+        g_rows0 = rows_then_xm.tile([P, PACK, HALF], BF16, name="g_rows0", offset=0, align_bytes=64)
+        for t in range(PACK):
+            nc.vector.tensor_scalar(g_rows0[:, t, :], resid0[:, t, :], w_lo[:, t:t + 1], w_hi[:, t:t + 1], ALU.max, ALU.min)
+        grouped = {}
+        for k in range(2):
+            tile = held.tile([P, P, PACK], BF16, name="block_grouped%d" % k, align_bytes=64)
+            grouped.setdefault(k, interleave_block(nc.scalar.copy, k, tile[:]))
+        g_grouped0 = held.tile([P, HALF, PACK], BF16, name="g_grouped0", tag="g_grouped0", align_bytes=64)
+        interleave(nc.scalar.copy, g_grouped0[:, G_SHARE:], g_rows0[:, :, G_SHARE:])
+
+        blocks = quantize_blocks(0, grouped[0])
+        interleave(nc.vector.tensor_copy, g_grouped0[:, :G_SHARE], g_rows0[:, :, :G_SHARE])
+        for k in range(2, 4):
+            tile = rows_then_xm.tile([P, P, PACK], BF16, name="block_grouped%d" % k, offset=(k % 2) * P * PACK * 2, align_bytes=64)
+            grouped.setdefault(k, interleave_block(nc.scalar.copy, k, tile[:]))
+        resid1 = held.tile([P, PACK, HALF], F32, name="resid1", tag="resid")
+        nc.vector.tensor_tensor(resid1[:, :2, :], scores1[0][:], targets[:, :2, HALF:], ALU.subtract)
+        quantize_g(0, g_grouped0[:])
         early = [early_half(0)]
+        nc.vector.tensor_tensor(resid1[:, 2:, :], scores1[1][:], late_targets[:], ALU.subtract)
+        blocks.extend(quantize_blocks(1, grouped[1]))
         scatter_early(0)
-
-        g_grouped1, g_copy1 = gradient_rows(1)
-        nc.vector.tensor_copy(*g_copy1)
-        quantize_g(1, g_grouped1)
-        blocks.extend(quantize_blocks(1, 1, grouped))
         early.append(early_half(1))
-        grouped = interleave_blocks(nc.vector.tensor_copy, 2, 2, held_blocks(2, 2, "g_rows1"))
-        late = [late_half(0)]
-        blocks.extend(quantize_blocks(2, 2, grouped))
-        late.append(late_half(1))
 
-        for k in range(0, PACK, 2):
-            by_scalar = interleave_blocks(nc.scalar.copy, k + 4, 1, held_blocks(k + 4, 1, "early%d" % EARLY_SLOT[k]))
-            scatter_late(k)
-            scales = stage.tile([P, P], U8, name="block_scales%d" % (k + 4), offset=LATE_AT[k] + 256, align_bytes=64)
-            blocks.extend(quantize_blocks(k + 4, 1, by_scalar, scales))
-            by_vector = stage.tile([P, P, PACK], BF16, name="block_grouped%d" % (k + 5), offset=LATE_AT[k] - 768, align_bytes=64)
-            interleave_blocks(nc.vector.tensor_copy, k + 5, 1, by_vector)
-            late.append(late_half(k + 2))
-            blocks.extend(quantize_blocks(k + 5, 1, by_vector))
-            if k == 0:
-                scatter_early(1)
-                early.extend([early_half(2), early_half(3)])
-                scatter_early(2)
-            else:
-                early.append(early_half(4))
-                scatter_early(3)
-                early.append(early_half(5))
-                scatter_early(4)
-            scatter_late(k + 1)
-            late.append(late_half(k + 3))
-        for k in range(PACK, D // P):
-            if k + 2 < D // P:
-                early.append(early_half(k + 2))
-            if k + 1 < D // P:
+        quarters = [slice(q * P, (q + 1) * P) for q in range(2)]
+        clipped = held.tile([P, HALF, PACK], F32, name="clipped", tag="g_grouped0", align_bytes=64)
+        for items in quarters:
+            nc.vector.tensor_scalar(clipped[:, items].rearrange("p (e i) t -> p e t i", i=4), resid1[:, :, items].rearrange("p t (e i) -> p e t i", i=4), -1.0, 1.0, ALU.max, ALU.min)
+        g_grouped1 = held.tile([P, HALF, PACK], BF16, name="g_grouped1", align_bytes=64)
+        for items in quarters:
+            nc.vector.tensor_tensor(g_grouped1[:, items], clipped[:, items], w_row[:].unsqueeze(1).to_broadcast([P, P, PACK]), ALU.mult)
+        for q, items in enumerate(quarters):
+            quantize_g(HALF + q * P, g_grouped1[:, items])
+        late_scales = held.tile([P, 2 * P], U8, name="late_scales", tag="g_grouped0", align_bytes=64)
+        blocks.extend(quantize_blocks(2, grouped[2], late_scales[:, :P]))
+
+        fifth = scalar_stage.tile([P, P, PACK], BF16, name="block_grouped5", offset=0, align_bytes=64)
+        interleave_block(nc.scalar.copy, 5, fifth[:])
+        late = [late_half(0)]
+        blocks.extend(quantize_blocks(3, grouped[3], late_scales[:, P:]))
+        scatter_early(1)
+        early.extend([early_half(2), early_half(3)])
+        scatter_late(0)
+
+        def scale_plane(k, at):
+            return vector_stage.tile([P, P], U8, name="block_scales%d" % k, offset=at, align_bytes=64)
+
+        by_vector = vector_stage.tile([P, P, PACK], BF16, name="block_grouped4", offset=64, align_bytes=64)
+        interleave_block(nc.vector.tensor_copy, 4, by_vector[:])
+        late.append(late_half(1))
+        blocks.extend(quantize_blocks(4, by_vector[:]))
+        late.append(late_half(2))
+        scatter_early(2)
+        sixth = scalar_stage.tile([P, P, PACK], BF16, name="block_grouped6", offset=2112, align_bytes=64)
+        interleave_block(nc.scalar.copy, 6, sixth[:])
+        early.append(early_half(4))
+        scatter_late(1)
+
+        blocks.extend(quantize_blocks(5, fifth[:], scale_plane(5, 1152)))
+        late.append(late_half(3))
+        scatter_early(3)
+        last = scalar_stage.tile([P, P, PACK], BF16, name="block_grouped7", offset=64, align_bytes=64)
+        interleave_block(nc.scalar.copy, 7, last[:])
+        early.append(early_half(5))
+        scatter_late(2)
+
+        blocks.extend(quantize_blocks(6, sixth[:], scale_plane(6, 2880 + 64)))
+        late.append(late_half(4))
+        scatter_early(4)
+        early.append(early_half(6))
+        scatter_late(3)
+
+        blocks.extend(quantize_blocks(7, last[:], scale_plane(7, 4224)))
+        late.extend([late_half(5), late_half(6)])
+        scatter_early(5)
+        early.append(early_half(7))
+        scatter_late(4)
+        late.append(late_half(7))
+        for k in range(5, BLOCKS):
+            if k + 1 < BLOCKS:
                 scatter_early(k + 1)
             scatter_late(k)
-            if k + 2 < D // P:
-                late.append(late_half(k + 2))

@@ -24,8 +24,9 @@ BLOCKS = D // P
 HALF = N // 2
 WINDOWS = 4
 G_SHARE = 48
+SCALAR_SHARE = (256, 256, 256, 256, 256, 256, 256, 384)
 EARLY_AT = (0, 1024, 3072, 1024, 4032, 1088, 4032, 1088)
-LATE_AT = (1024, 3072, 1984, 4032, 1920, 3072, 4992, 1920)
+LATE_AT = (1024, 3072, 1984, 4032, 1920, 3072, 4992, 3072)
 XM_CHUNKS = ((0, 256), (256, 256), (512, 512))
 
 
@@ -62,6 +63,8 @@ def tile_attend_ghub_w_kernel(tc, xT, w_words, w_scales, y, wt, xm, offs, out):
 
         moved_scales = held.tile([P, N // 4], I32, name="moved_scales", align_bytes=64)
         nc.vector.memset(moved_scales[:], 0)
+        zeros = held.tile([P, N - SCALAR_SHARE[-1]], F32, name="zeros")
+        nc.vector.memset(zeros[:], 0.0)
         windows = [held.tile([P, T], F32, name="window%d" % k) for k in range(WINDOWS)]
 
         def zero(k, first, count):
@@ -121,8 +124,6 @@ def tile_attend_ghub_w_kernel(tc, xT, w_words, w_scales, y, wt, xm, offs, out):
         pairs = [gather_pairs(h) for h in range(2)]
         item_words = [part_pairs(h, pairs[h]) for h in range(2)]
         x_operands = [quantize_x(0, 0, 2)]
-        zero(WINDOWS - 1, T // 2, T // 2)
-        x_operands[0].extend(quantize_x(0, 2, 2))
 
         xm_rows = xm[0].rearrange("(p t) d -> p t d", t=PACK)
         xm_raw = []
@@ -156,6 +157,9 @@ def tile_attend_ghub_w_kernel(tc, xT, w_words, w_scales, y, wt, xm, offs, out):
         for piece in range(2):
             deal(nc.vector.tensor_copy, x_raw[2 + piece], 1, 0, 2 * piece)
             deal(nc.scalar.copy, x_raw[2 + piece], 1, 1, 2 * piece)
+            if piece == 0:
+                x_operands[0].extend(quantize_x(0, 2, 2))
+            zero(WINDOWS - 1, T // 2 + piece * T // 4, T // 4)
         x_operands.append(quantize_x(1, 0, 1) + quantize_x(1, 1, 1) + quantize_x(1, 2, 2))
         for g in range(PASSES):
             for t in range(PACK):
@@ -207,26 +211,34 @@ def tile_attend_ghub_w_kernel(tc, xT, w_words, w_scales, y, wt, xm, offs, out):
             )
             return grad
 
-        def places(k, h):
-            return windows[k % WINDOWS][:].indirect(entries(h * HALF, HALF))
+        def places(k, first, count):
+            return windows[k % WINDOWS][:].indirect(entries(first, count))
+
+        banks = {}
 
         def early_half(k):
-            grad = second_product(2 + k % 2, blocks[k], 0, HALF)
-            dense = scalar_stage.tile([P, HALF], F32, name="early%d" % k, offset=EARLY_AT[k], align_bytes=64)
-            nc.scalar.copy(dense[:], grad[:])
+            share = SCALAR_SHARE[k]
+            banks.setdefault(k, second_product(2 + k % 3, blocks[k], 0, HALF if share == HALF else N))
+            dense = scalar_stage.tile([P, share], F32, name="early%d" % k, offset=EARLY_AT[k], align_bytes=64)
+            nc.scalar.copy(dense[:], banks[k][:, :share])
             return dense
 
         def late_half(k):
-            grad = second_product(5 + k % 3, blocks[k], HALF, HALF)
-            dense = vector_stage.tile([P, HALF], F32, name="late%d" % k, offset=LATE_AT[k], align_bytes=64)
-            nc.vector.tensor_copy(dense[:], grad[:])
+            share = SCALAR_SHARE[k]
+            sums = second_product(5 + k % 3, blocks[k], HALF, HALF)[:] if share == HALF else banks[k][:, share:]
+            dense = vector_stage.tile([P, N - share], F32, name="late%d" % k, offset=LATE_AT[k], align_bytes=64)
+            nc.vector.tensor_copy(dense[:], sums)
             return dense
 
         def scatter_early(k):
-            nc.scalar.activation(places(k, 0), early[k][:], ACT.Copy)
+            nc.scalar.activation(places(k, 0, SCALAR_SHARE[k]), early[k][:], ACT.Copy)
 
         def scatter_late(k):
-            nc.vector.tensor_copy(places(k, 1), late[k][:])
+            share = SCALAR_SHARE[k]
+            if share == HALF:
+                nc.vector.tensor_copy(places(k, HALF, HALF), late[k][:])
+            else:
+                nc.vector.tensor_tensor(places(k, share, N - share), late[k][:], zeros[:, :N - share], ALU.add)
             nc.sync.dma_start(out[k * P:(k + 1) * P, :], windows[k % WINDOWS][:])
 
         resid0 = held.tile([P, PACK, HALF], F32, name="resid0", tag="resid")
@@ -309,8 +321,9 @@ def tile_attend_ghub_w_kernel(tc, xT, w_words, w_scales, y, wt, xm, offs, out):
         scatter_early(5)
         early.append(early_half(7))
         scatter_late(4)
+        scatter_early(6)
+        scatter_late(5)
         late.append(late_half(7))
-        for k in range(5, BLOCKS):
-            if k + 1 < BLOCKS:
-                scatter_early(k + 1)
-            scatter_late(k)
+        scatter_early(7)
+        scatter_late(6)
+        scatter_late(7)

from contextlib import ExitStack

import concourse.mybir as mybir

N, T, D, R = 512, 2048, 1024, 512
FLOPS = 2 * 2 * D * R * N

F32 = mybir.dt.float32
BF16 = mybir.dt.bfloat16
I32 = mybir.dt.int32
U32 = mybir.dt.uint32
U16 = mybir.dt.uint16
U8 = mybir.dt.uint8
E4M3 = mybir.dt.float8_e4m3fn_x4
E5M2 = mybir.dt.float8_e5m2_x4
E2M1 = mybir.dt.float4_e2m1fn_x4
ALU = mybir.AluOpType
ACT = mybir.ActivationFunctionType

P = 128
PACK = 4
PASSES = D // (P * PACK)
BLOCKS = D // P
HALF = N // 2
WINDOWS = 4
G_SHARE = 48
SCALAR_SHARE = (256, 256, 256, 256, 256, 256, 256, 384)
EARLY_AT = (0, 1024, 3072, 1024, 4032, 1088, 4032, 1088)
LATE_AT = (1024, 3072, 1984, 4032, 1920, 3072, 4992, 3072)
XM_CHUNKS = ((0, 256), (256, 256), (512, 512))


def tile_attend_ghub_w_kernel(tc, xT, w_words, w_scales, y, wt, xm, offs, out):
    nc = tc.nc
    with ExitStack() as ctx:
        held = ctx.enter_context(tc.tile_pool(name="held", bufs=1))
        words_then_xm = ctx.enter_context(tc.tile_pool(name="words_then_xm", bufs=1))
        rows_then_xm = ctx.enter_context(tc.tile_pool(name="rows_then_xm", bufs=1))
        scalar_stage = ctx.enter_context(tc.tile_pool(name="scalar_stage", bufs=1))
        vector_stage = ctx.enter_context(tc.tile_pool(name="vector_stage", bufs=1))
        psum = ctx.enter_context(tc.psum_pool(name="psum", bufs=1))

        def load_x(g, first, count):
            raw = held.tile([P, count, R], F32, name="x_raw%d_%d" % (g, first), tag="x_raw%d_%d" % (g, first))
            rows = xT[0, g * 512:(g + 1) * 512, :].rearrange("(p j) r -> p j r", j=PACK)
            nc.sync.dma_start(raw[:], rows[:, first:first + count, :])
            return raw

        x_raw = [load_x(0, 0, 2)]
        offsets = held.tile([P, N // 16], U16, name="offsets")
        nc.sync.dma_start(offsets[:], offs)
        table_scales = held.tile([P, T // 4], I32, name="table_scales", tag="scales_then_y", align_bytes=64)
        nc.vector.memset(table_scales[:], 0)
        scale_rows = w_scales.bitcast(I32).rearrange("o (q b) t -> b q o t", b=4)
        for b in range(4):
            nc.sync.dma_start(table_scales[b:P:16, :], scale_rows[b])
        table_words = words_then_xm.tile([P, T], I32, name="table_words", offset=0, align_bytes=64)
        nc.sync.dma_start(table_words[:], w_words[0].rearrange("p t b -> p (t b)").bitcast(I32))
        x_raw.extend([load_x(0, 2, 2), load_x(1, 0, 2), load_x(1, 2, 2)])

        w_row = held.tile([P, PACK], F32, name="w_row")
        nc.sync.dma_start(w_row[:], wt[0].rearrange("(p t) o -> p (t o)", t=PACK))

        moved_scales = held.tile([P, N // 4], I32, name="moved_scales", align_bytes=64)
        nc.vector.memset(moved_scales[:], 0)
        zeros = held.tile([P, N - SCALAR_SHARE[-1]], F32, name="zeros")
        nc.vector.memset(zeros[:], 0.0)
        windows = [held.tile([P, T], F32, name="window%d" % k) for k in range(WINDOWS)]

        def zero(k, first, count):
            nc.vector.memset(windows[k][:, first:first + count].bitcast(I32), 0)

        for k in range(WINDOWS - 1):
            zero(k, 0, T)

        x_grouped = [[held.tile([P, 2, P, PACK], BF16, name="x_grouped%d_%d" % (g, u), align_bytes=64) for u in range(2)] for g in range(PASSES)]

        def deal(copy, raw, g, u, first):
            src = raw[:].rearrange("p j (m t) -> p m j t", t=PACK)[:, :, :, 2 * u:2 * u + 2]
            copy(x_grouped[g][u][:].rearrange("p t m j -> p m j t")[:, :, first:first + src.shape[2]], src)

        def quantize(name, grouped, scales=None):
            width = grouped.shape[1] // PACK
            codes = held.tile([P, width], U32, name=name + "_codes", align_bytes=64)
            if scales is None:
                scales = held.tile([P, width], U8, name=name + "_scales", align_bytes=64)
            nc.vector.quantize_mx(codes[:].bitcast(E4M3), scales[:, :], grouped)
            return [(codes[:, c:c + P], scales[:, c:c + P]) for c in range(0, width, P)]

        def quantize_x(g, first, count):
            u, v = divmod(first, 2)
            return quantize("x%d_%d" % (g, first), x_grouped[g][u][:, v:v + count].rearrange("p t m j -> p (t m j)"))

        def entries(first, count):
            return offsets[:, first // 16:(first + count) // 16]

        for u in range(2):
            deal(nc.scalar.copy, x_raw[0], 0, u, 0)
        for u in range(2):
            deal(nc.scalar.copy, x_raw[1], 0, u, 2)

        both_scales = held.tile([P, N], U8, name="both_scales", align_bytes=64)
        nc.vector.tensor_copy(both_scales[:], table_scales[:].bitcast(U8).indirect(offsets[:]))
        for first, count in ((0, 64), (64, 4), (96, 4)):
            nc.sync.dma_start(moved_scales[first:first + count, :], both_scales[first + 16:first + 16 + count, :].bitcast(I32))
        item_scales = [both_scales[:], moved_scales[:].bitcast(U8)]

        targets = held.tile([P, PACK, N], F32, name="targets", tag="scales_then_y", align_bytes=64)
        y_rows = y[0].rearrange("(p t) i -> p t i", t=PACK)
        nc.sync.dma_start(targets[:, :2, :], y_rows[:, :2, :])
        nc.sync.dma_start(targets[:, 2:, :HALF], y_rows[:, 2:, :HALF])

        def gather_pairs(h):
            pairs = held.tile([P, HALF], U32, name="item_pairs%d" % h, tag="item_pairs%d" % h, align_bytes=64)
            nc.vector.tensor_copy(pairs[:], table_words[:].bitcast(U32).indirect(entries(h * HALF, HALF)))
            return pairs

        def part_pairs(h, pairs):
            words = held.tile([P, PASSES, HALF], U16, name="item_words%d" % h, align_bytes=64)
            nc.vector.tensor_copy(words[:], pairs[:].bitcast(U16).rearrange("p (n o) -> p o n", o=PASSES))
            return words

        zero(WINDOWS - 1, 0, T // 2)
        pairs = [gather_pairs(h) for h in range(2)]
        item_words = [part_pairs(h, pairs[h]) for h in range(2)]
        x_operands = [quantize_x(0, 0, 2)]

        xm_rows = xm[0].rearrange("(p t) d -> p t d", t=PACK)
        xm_raw = []
        for c, (first, width) in enumerate(XM_CHUNKS):
            if c < 2:
                raw = words_then_xm.tile([P, PACK, width], F32, name="xm_raw%d" % c, offset=first * PACK * 4, align_bytes=64)
            else:
                raw = held.tile([P, PACK, width], F32, name="xm_raw%d" % c, tag="x_raw1_2")
            xm_raw.append(raw)

        def load_xm(c):
            first, width = XM_CHUNKS[c]
            nc.sync.dma_start(xm_raw[c][:], xm_rows[:, :, first:first + width])

        load_xm(0)
        late_targets = held.tile([P, 2, HALF], F32, name="late_targets", tag="item_pairs1", align_bytes=64)
        nc.sync.dma_start(late_targets[:], y_rows[:, 2:, HALF:])
        load_xm(1)

        scores0 = [psum.tile([P, HALF], F32, name="scores0_%d" % t, tag="bank%d" % t) for t in range(PACK)]
        scores1 = [psum.tile([P, 2, HALF], F32, name="scores1_%d" % u, tag="bank%d" % (PACK, 0)[u]) for u in range(2)]

        def first_product(g, h, t, sums, opens, closes):
            nc.tensor.matmul_mx(
                sums,
                lhsT=x_operands[g][t][0].bitcast(E4M3), lhsT_scale=x_operands[g][t][1],
                rhs=item_words[h][:, g, :].bitcast(E2M1), rhs_scale=item_scales[g][:, h * HALF:(h + 1) * HALF],
                start=opens, stop=closes,
            )

        for piece in range(2):
            deal(nc.vector.tensor_copy, x_raw[2 + piece], 1, 0, 2 * piece)
            deal(nc.scalar.copy, x_raw[2 + piece], 1, 1, 2 * piece)
            if piece == 0:
                x_operands[0].extend(quantize_x(0, 2, 2))
            zero(WINDOWS - 1, T // 2 + piece * T // 4, T // 4)
        x_operands.append(quantize_x(1, 0, 1) + quantize_x(1, 1, 1) + quantize_x(1, 2, 2))
        for g in range(PASSES):
            for t in range(PACK):
                first_product(g, 0, t, scores0[t][:], g == 0, g == PASSES - 1)
        for u in range(2):
            for g in range(PASSES):
                for v in range(2):
                    first_product(g, 1, 2 * u + v, scores1[u][:, v, :], (g, v) == (0, 0), (g, v) == (PASSES - 1, 1))
        load_xm(2)

        w_hi = held.tile([P, PACK], F32, name="w_hi")
        w_lo = held.tile([P, PACK], F32, name="w_lo")
        nc.scalar.activation(w_hi[:], w_row[:], ACT.Abs)
        nc.scalar.activation(w_lo[:], w_hi[:], ACT.Copy, scale=-1.0)

        weighted = []
        for t in range(PACK):
            yw = held.tile([P, HALF], F32, name="yw%d" % t, align_bytes=64)
            nc.scalar.activation(yw[:], targets[:, t, :HALF], ACT.Copy, scale=w_row[:, t:t + 1])
            weighted.append(yw)

        def interleave(copy, grouped, rows):
            copy(grouped.rearrange("p (e i) t -> p e t i", i=4), rows.rearrange("p t (e i) -> p e t i", i=4))
            return grouped

        def interleave_block(copy, k, grouped):
            c = max(j for j in range(len(XM_CHUNKS)) if XM_CHUNKS[j][0] <= k * P)
            first = k * P - XM_CHUNKS[c][0]
            return interleave(copy, grouped, xm_raw[c][:, :, first:first + grouped.shape[1]])

        def quantize_blocks(k, grouped, scales=None):
            return quantize("block%d" % k, grouped.rearrange("p d t -> p (d t)"), scales)

        g_codes = held.tile([P, N], U32, name="g_codes", align_bytes=64)
        g_scales = held.tile([P, N], U8, name="g_scales", align_bytes=64)

        def quantize_g(first, grouped):
            items = slice(first, first + grouped.shape[1])
            nc.vector.quantize_mx(g_codes[:, items].bitcast(E5M2), g_scales[:, items], grouped.rearrange("p i t -> p (i t)"))

        def second_product(bank, block, first, count):
            items = slice(first, first + count)
            grad = psum.tile([P, count], F32, name="grad", tag="bank%d" % bank)
            nc.tensor.matmul_mx(
                grad[:],
                lhsT=block[0].bitcast(E4M3), lhsT_scale=block[1],
                rhs=g_codes[:, items].bitcast(E5M2), rhs_scale=g_scales[:, items],
                start=True, stop=True,
            )
            return grad

        def places(k, first, count):
            return windows[k % WINDOWS][:].indirect(entries(first, count))

        banks = {}

        def early_half(k):
            share = SCALAR_SHARE[k]
            banks.setdefault(k, second_product(2 + k % 3, blocks[k], 0, HALF if share == HALF else N))
            dense = scalar_stage.tile([P, share], F32, name="early%d" % k, offset=EARLY_AT[k], align_bytes=64)
            nc.scalar.copy(dense[:], banks[k][:, :share])
            return dense

        def late_half(k):
            share = SCALAR_SHARE[k]
            sums = second_product(5 + k % 3, blocks[k], HALF, HALF)[:] if share == HALF else banks[k][:, share:]
            dense = vector_stage.tile([P, N - share], F32, name="late%d" % k, offset=LATE_AT[k], align_bytes=64)
            nc.vector.tensor_copy(dense[:], sums)
            return dense

        def scatter_early(k):
            nc.scalar.activation(places(k, 0, SCALAR_SHARE[k]), early[k][:], ACT.Copy)

        def scatter_late(k):
            share = SCALAR_SHARE[k]
            if share == HALF:
                nc.vector.tensor_copy(places(k, HALF, HALF), late[k][:])
            else:
                nc.vector.tensor_tensor(places(k, share, N - share), late[k][:], zeros[:, :N - share], ALU.add)
            nc.sync.dma_start(out[k * P:(k + 1) * P, :], windows[k % WINDOWS][:])

        resid0 = held.tile([P, PACK, HALF], F32, name="resid0", tag="resid")
        for t in range(PACK):
            nc.vector.scalar_tensor_tensor(resid0[:, t, :], scores0[t][:], w_row[:, t:t + 1], weighted[t][:], ALU.mult, ALU.subtract)
        g_rows0 = rows_then_xm.tile([P, PACK, HALF], BF16, name="g_rows0", offset=0, align_bytes=64)
        for t in range(PACK):
            nc.vector.tensor_scalar(g_rows0[:, t, :], resid0[:, t, :], w_lo[:, t:t + 1], w_hi[:, t:t + 1], ALU.max, ALU.min)
        grouped = {}
        for k in range(2):
            tile = held.tile([P, P, PACK], BF16, name="block_grouped%d" % k, align_bytes=64)
            grouped.setdefault(k, interleave_block(nc.scalar.copy, k, tile[:]))
        g_grouped0 = held.tile([P, HALF, PACK], BF16, name="g_grouped0", tag="g_grouped0", align_bytes=64)
        interleave(nc.scalar.copy, g_grouped0[:, G_SHARE:], g_rows0[:, :, G_SHARE:])

        blocks = quantize_blocks(0, grouped[0])
        interleave(nc.vector.tensor_copy, g_grouped0[:, :G_SHARE], g_rows0[:, :, :G_SHARE])
        for k in range(2, 4):
            tile = rows_then_xm.tile([P, P, PACK], BF16, name="block_grouped%d" % k, offset=(k % 2) * P * PACK * 2, align_bytes=64)
            grouped.setdefault(k, interleave_block(nc.scalar.copy, k, tile[:]))
        resid1 = held.tile([P, PACK, HALF], F32, name="resid1", tag="resid")
        nc.vector.tensor_tensor(resid1[:, :2, :], scores1[0][:], targets[:, :2, HALF:], ALU.subtract)
        quantize_g(0, g_grouped0[:])
        early = [early_half(0)]
        nc.vector.tensor_tensor(resid1[:, 2:, :], scores1[1][:], late_targets[:], ALU.subtract)
        blocks.extend(quantize_blocks(1, grouped[1]))
        scatter_early(0)
        early.append(early_half(1))

        quarters = [slice(q * P, (q + 1) * P) for q in range(2)]
        clipped = held.tile([P, HALF, PACK], F32, name="clipped", tag="g_grouped0", align_bytes=64)
        for items in quarters:
            nc.vector.tensor_scalar(clipped[:, items].rearrange("p (e i) t -> p e t i", i=4), resid1[:, :, items].rearrange("p t (e i) -> p e t i", i=4), -1.0, 1.0, ALU.max, ALU.min)
        g_grouped1 = held.tile([P, HALF, PACK], BF16, name="g_grouped1", align_bytes=64)
        for items in quarters:
            nc.vector.tensor_tensor(g_grouped1[:, items], clipped[:, items], w_row[:].unsqueeze(1).to_broadcast([P, P, PACK]), ALU.mult)
        for q, items in enumerate(quarters):
            quantize_g(HALF + q * P, g_grouped1[:, items])
        late_scales = held.tile([P, 2 * P], U8, name="late_scales", tag="g_grouped0", align_bytes=64)
        blocks.extend(quantize_blocks(2, grouped[2], late_scales[:, :P]))

        fifth = scalar_stage.tile([P, P, PACK], BF16, name="block_grouped5", offset=0, align_bytes=64)
        interleave_block(nc.scalar.copy, 5, fifth[:])
        late = [late_half(0)]
        blocks.extend(quantize_blocks(3, grouped[3], late_scales[:, P:]))
        scatter_early(1)
        early.extend([early_half(2), early_half(3)])
        scatter_late(0)

        def scale_plane(k, at):
            return vector_stage.tile([P, P], U8, name="block_scales%d" % k, offset=at, align_bytes=64)

        by_vector = vector_stage.tile([P, P, PACK], BF16, name="block_grouped4", offset=64, align_bytes=64)
        interleave_block(nc.vector.tensor_copy, 4, by_vector[:])
        late.append(late_half(1))
        blocks.extend(quantize_blocks(4, by_vector[:]))
        late.append(late_half(2))
        scatter_early(2)
        sixth = scalar_stage.tile([P, P, PACK], BF16, name="block_grouped6", offset=2112, align_bytes=64)
        interleave_block(nc.scalar.copy, 6, sixth[:])
        early.append(early_half(4))
        scatter_late(1)

        blocks.extend(quantize_blocks(5, fifth[:], scale_plane(5, 1152)))
        late.append(late_half(3))
        scatter_early(3)
        last = scalar_stage.tile([P, P, PACK], BF16, name="block_grouped7", offset=64, align_bytes=64)
        interleave_block(nc.scalar.copy, 7, last[:])
        early.append(early_half(5))
        scatter_late(2)

        blocks.extend(quantize_blocks(6, sixth[:], scale_plane(6, 2880 + 64)))
        late.append(late_half(4))
        scatter_early(4)
        early.append(early_half(6))
        scatter_late(3)

        blocks.extend(quantize_blocks(7, last[:], scale_plane(7, 4224)))
        late.extend([late_half(5), late_half(6)])
        scatter_early(5)
        early.append(early_half(7))
        scatter_late(4)
        scatter_early(6)
        scatter_late(5)
        late.append(late_half(7))
        scatter_early(7)
        scatter_late(6)
        scatter_late(7)
